import numpy as np
import ml_dtypes


def mxq(x, axis, fmt="e4m3"):
    dtype, down = {"e4m3": (ml_dtypes.float8_e4m3fn, 7), "e5m2": (ml_dtypes.float8_e5m2, 14)}[fmt]
    v = np.moveaxis(np.asarray(x, np.float32).astype(ml_dtypes.bfloat16).astype(np.float64), axis, -1)
    blocks = v.reshape(v.shape[:-1] + (-1, 32))
    amax = np.abs(blocks).max(-1, keepdims=True)
    byte = np.maximum(np.where(amax > 0, np.frexp(amax)[1] - 1 + 127, 0) - down, 1)
    scale = np.exp2(byte - 127.0)
    codes = (blocks / scale).astype(np.float32).astype(dtype).astype(np.float64)
    return np.moveaxis((codes * scale).reshape(v.shape), -1, axis)


WIDE = False


def mx_kscale(k):
    if not WIDE:
        return np.ones(k)
    levels = np.array([10, -10, 5, -5, 0])
    if k % 512:
        return np.exp2(np.random.permutation(np.resize(levels, k // 32))).repeat(32)
    a = np.empty((k // 512, 16))
    for p in range(k // 512):
        a[p, :8] = np.random.permutation(np.resize(levels, 8))
        for g in range(8):
            far = levels[np.abs(levels - a[p, g]) >= 10]
            a[p, g + 8] = far[np.random.randint(len(far))]
    return np.exp2(a.ravel()).repeat(32)


def f64(x):
    return np.asarray(x).astype(np.float64)


def striped8(idx):
    return np.asarray(idx).reshape(8, -1, 16).transpose(0, 2, 1).reshape(128, -1).astype(np.uint16)


def unstriped8(offs):
    return offs.reshape(8, 16, -1).transpose(0, 2, 1).reshape(8, -1).astype(np.int64)


def pick8(x, idx, run):
    r = np.arange(len(x))
    return x[r[:, None], idx[r % (8 * run) // run]]


def bf(x):
    return np.asarray(x, np.float32).astype(ml_dtypes.bfloat16)


def planes(Y):
    r, m = Y.shape
    b = f64(bf(Y)).reshape(r // 32, 32, m)
    amax = np.abs(b).max(1)
    byte = np.clip(np.where(amax > 0, np.frexp(amax)[1] - 1 + 127 - 7, 1), 1, 254)
    codes = (b * np.exp2(127.0 - byte)[:, None, :]).reshape(r, m).astype(np.float32).astype(ml_dtypes.float8_e4m3fn).view(np.uint8)
    words = codes.reshape(r // 512, 128, 4, m).transpose(0, 1, 3, 2)
    return np.ascontiguousarray(words), np.ascontiguousarray(byte.astype(np.uint8).reshape(r // 512, 16, m))


D, T, J, C = 512, 2048, 512, 512


def setup_inputs():
    n = np.random.standard_normal
    idx = np.stack([np.random.permutation(T)[:J] for _ in range(8)])
    idx2 = np.stack([np.random.permutation(T)[:J] for _ in range(8)])
    fd = mx_kscale(D)
    return {
        "keys": (n((D, T)) / fd[:, None]).astype(np.float32),
        "ka": (np.random.uniform(0.5, 1.0, (1, J))).astype(np.float32),
        "kb": (np.random.uniform(0.2, 0.7, (1, J))).astype(np.float32),
        "wd": (n((D, C)) * 1 / np.sqrt(D) * fd[:, None]).astype(np.float32),
        "offs": striped8(idx),
        "offs2": striped8(idx2),
    }


def reference(keys, ka, kb, wd, offs, offs2):
    idx = unstriped8(offs)
    idx2 = unstriped8(offs2)
    x = pick8(f64(keys), idx, 64) * f64(ka) + pick8(f64(keys), idx2, 64) * f64(kb)
    wdq = mxq(f64(wd), 0, "e4m3")
    xq = mxq(x, 0, "e4m3")
    y = wdq.T @ xq
    words, scales = planes(y)
    return y, words, scales

@@ -1,0 +1,178 @@
+from contextlib import ExitStack
+
+import concourse.mybir as mybir
+from concourse.masks import make_identity
+
+D, T, J, C = 512, 2048, 512, 512
+FLOPS = 2 * D * C * J
+
+F32 = mybir.dt.float32
+BF16 = mybir.dt.bfloat16
+I32 = mybir.dt.int32
+U16 = mybir.dt.uint16
+U8 = mybir.dt.uint8
+FP8X4 = mybir.dt.float8_e4m3fn_x4
+MULT = mybir.AluOpType.mult
+ADD = mybir.AluOpType.add
+
+P = 128
+PACK = 4
+CH = 128
+NCH = J // CH
+LINE = 4
+
+
+def tile_attend_headmerge_pl_kernel(tc, keys, ka, kb, wd, offs, offs2, out_0, out_1, out_2):
+    nc = tc.nc
+    with ExitStack() as ctx:
+        keep = ctx.enter_context(tc.tile_pool(name="keep", bufs=1))
+        psum = ctx.enter_context(tc.psum_pool(name="psum", bufs=1))
+
+        list_a = keep.tile([P, J // 16], U16, name="list_a")
+        list_b = keep.tile([P, J // 16], U16, name="list_b")
+        planes = [keep.tile([P, T], F32, name=f"plane{t}") for t in range(PACK)]
+        key_rows = keys.rearrange("(p t) n -> p t n", t=PACK)
+        w_rows = wd.rearrange("(p r) c -> p r c", r=PACK)
+        w_raw = [keep.tile([P, PACK, C // 2], F32, name=f"w_raw{h}") for h in range(2)]
+        cols = [keep.tile([P, PACK], F32, name=f"share_cols{s}") for s in range(2)]
+
+        nc.sync.dma_start(out=planes[0][:], in_=key_rows[:, 0, :])
+        nc.sync.dma_start(list_a[:], offs)
+        nc.sync.dma_start(list_b[:], offs2)
+        for s, share in enumerate((ka, kb)):
+            nc.scalar.dma_start(out=cols[s][:], in_=share.rearrange("o (p i) -> p (o i)", i=PACK))
+        for t in range(1, PACK):
+            nc.sync.dma_start(out=planes[t][:], in_=key_rows[:, t, :])
+        for h in range(2):
+            nc.sync.dma_start(out=w_raw[h][:], in_=w_rows[:, :, h * (C // 2) : (h + 1) * (C // 2)])
+
+        ident = keep.tile([P, P], F32, name="ident")
+        make_identity(nc, ident[:])
+        shares = []
+        for s in range(2):
+            spread = psum.tile([P, PACK, P], F32, name=f"spread{s}")
+            for i in range(PACK):
+                nc.tensor.transpose(spread[:, i, :], cols[s][:, i : i + 1].to_broadcast([P, P]), ident[:])
+            row = keep.tile([P, J], F32, name=f"share{s}")
+            dst = row[:].rearrange("m (p i) -> m p i", i=PACK)
+            src = spread[:].rearrange("m i p -> m p i")
+            if s == 0:
+                nc.vector.tensor_copy(out=dst, in_=src)
+            else:
+                nc.scalar.copy(out=dst, in_=src)
+            shares.append(row)
+
+        terms = [keep.tile([P, PACK, J], F32, name=f"term{s}") for s in range(2)]
+        lists = (list_a, list_b)
+
+        def gather(t, j0, j1):
+            for s in range(2):
+                nc.vector.tensor_tensor(
+                    terms[s][:, t, j0:j1],
+                    planes[t][:].indirect(lists[s][:, j0 // 16 : j1 // 16]),
+                    shares[s][:, j0:j1],
+                    MULT,
+                )
+
+        x_bf = [keep.tile([P, CH, PACK], BF16, name=f"x_bf{c}", align_bytes=64) for c in range(NCH)]
+        x_codes = [keep.tile([P, CH], I32, name=f"x_codes{c}", align_bytes=64) for c in range(NCH)]
+        x_scales = [keep.tile([P, CH], U8, name=f"x_scales{c}", align_bytes=64) for c in range(NCH)]
+
+        def merge(c):
+            js = slice(c * CH, (c + 1) * CH)
+            nc.vector.tensor_tensor(
+                x_bf[c][:].rearrange("p (g i) t -> p g t i", i=LINE),
+                terms[0][:, :, js].rearrange("p t (g i) -> p g t i", i=LINE),
+                terms[1][:, :, js].rearrange("p t (g i) -> p g t i", i=LINE),
+                ADD,
+            )
+
+        def quant_x(c):
+            nc.vector.quantize_mx(
+                out=x_codes[c][:].bitcast(FP8X4), scales=x_scales[c][:], in_=x_bf[c][:].rearrange("p j t -> p (j t)")
+            )
+
+        w_bf = keep.tile([P, PACK, P, PACK], BF16, name="w_bf", align_bytes=64)
+        w_codes = keep.tile([P, C], I32, name="w_codes", align_bytes=64)
+        w_scales = keep.tile([P, C], U8, name="w_scales", align_bytes=64)
+        for h in range(2):
+            nc.scalar.copy(
+                out=w_bf[:, :, h * (P // 2) : (h + 1) * (P // 2), :].rearrange("p t m r -> p m r t"),
+                in_=w_raw[h][:].rearrange("p r (m t) -> p m r t", t=PACK),
+            )
+
+        def quant_w():
+            nc.vector.quantize_mx(
+                out=w_codes[:].bitcast(FP8X4), scales=w_scales[:], in_=w_bf[:].rearrange("p t m r -> p (t m r)")
+            )
+
+        acc = [psum.tile([P, PACK, CH], F32, name=f"acc{c}") for c in range(NCH)]
+        y = [keep.tile([P, PACK, CH], F32, name=f"y{c}") for c in range(NCH)]
+        y_bf = [keep.tile([P, CH, PACK], BF16, name=f"y_bf{c}", align_bytes=64) for c in range(NCH)]
+        y_codes = keep.tile([P, J], I32, name="y_codes", align_bytes=64)
+        y_scales = keep.tile([P, J], U8, name="y_scales", align_bytes=64)
+        y_rows = out_0.rearrange("(p t) j -> p t j", t=PACK)
+        word_rows = out_1[0].rearrange("l c r -> l (c r)").bitcast(I32)
+        scale_rows = out_2[0].bitcast(I32)
+
+        def project(c):
+            js = slice(c * CH, (c + 1) * CH)
+            for t in range(PACK):
+                ms = slice(t * P, (t + 1) * P)
+                nc.tensor.matmul_mx(
+                    out=acc[c][:, t, :],
+                    lhsT=w_codes[:, ms].bitcast(FP8X4),
+                    lhsT_scale=w_scales[:, ms],
+                    rhs=x_codes[c][:].bitcast(FP8X4),
+                    rhs_scale=x_scales[c][:],
+                    start=True,
+                    stop=True,
+                )
+            nc.scalar.copy(out=y[c][:], in_=acc[c][:])
+            nc.sync.dma_start(out=y_rows[:, :, js], in_=y[c][:])
+
+        def round_y(c):
+            nc.vector.tensor_copy(
+                out=y_bf[c][:].rearrange("p (g i) t -> p g t i", i=LINE),
+                in_=y[c][:].rearrange("p t (g i) -> p g t i", i=LINE),
+            )
+
+        def quant_y(c):
+            js = slice(c * CH, (c + 1) * CH)
+            nc.vector.quantize_mx(
+                out=y_codes[:, js].bitcast(FP8X4), scales=y_scales[:, js], in_=y_bf[c][:].rearrange("p j t -> p (j t)")
+            )
+
+        for t in range(PACK - 1):
+            gather(t, 0, J)
+        last = PACK - 1
+        gather(last, 0, CH)
+        gather(last, CH, 2 * CH)
+        merge(0)
+        gather(last, 2 * CH, 3 * CH)
+        quant_x(0)
+        merge(1)
+        gather(last, 3 * CH, 4 * CH)
+        quant_w()
+        quant_x(1)
+        project(0)
+        project(1)
+        merge(2)
+        merge(3)
+        quant_x(2)
+        project(2)
+        round_y(0)
+        quant_x(3)
+        project(3)
+        round_y(1)
+        quant_y(0)
+        round_y(2)
+        quant_y(1)
+        nc.sync.dma_start(out=word_rows[:, : J // 2], in_=y_codes[:, : J // 2])
+        round_y(3)
+        quant_y(2)
+        quant_y(3)
+        nc.sync.dma_start(out=word_rows[:, J // 2 :], in_=y_codes[:, J // 2 :])
+        for q in range(4):
+            queue = nc.scalar if q % 2 else nc.sync
+            queue.dma_start(out=scale_rows[4 * q : 4 * q + 4, :], in_=y_scales[32 * q : 32 * q + 4, :].bitcast(I32))

@@ -20,6 +20,7 @@ PACK = 4
 CH = 128
 NCH = J // CH
 LINE = 4
+W_PIECES = ((0, 256), (256, 384), (384, 512))
 
 
 def tile_attend_headmerge_pl_kernel(tc, keys, ka, kb, wd, offs, offs2, out_0, out_1, out_2):
@@ -33,18 +34,23 @@ def tile_attend_headmerge_pl_kernel(tc, keys, ka, kb, wd, offs, offs2, out_0, ou
         planes = [keep.tile([P, T], F32, name=f"plane{t}") for t in range(PACK)]
         key_rows = keys.rearrange("(p t) n -> p t n", t=PACK)
         w_rows = wd.rearrange("(p r) c -> p r c", r=PACK)
-        w_raw = [keep.tile([P, PACK, C // 2], F32, name=f"w_raw{h}") for h in range(2)]
+        w_raw = [keep.tile([P, PACK, c1 - c0], F32, name=f"w_raw{c0}") for c0, c1 in W_PIECES]
         cols = [keep.tile([P, PACK], F32, name=f"share_cols{s}") for s in range(2)]
 
+        def load_w(h):
+            nc.sync.dma_start(out=w_raw[h][:], in_=w_rows[:, :, W_PIECES[h][0] : W_PIECES[h][1]])
+
+        for s, share in enumerate((ka, kb)):
+            nc.sync.dma_start(out=cols[s][:], in_=share.rearrange("o (p i) -> p (o i)", i=PACK))
         nc.sync.dma_start(out=planes[0][:], in_=key_rows[:, 0, :])
         nc.sync.dma_start(list_a[:], offs)
         nc.sync.dma_start(list_b[:], offs2)
-        for s, share in enumerate((ka, kb)):
-            nc.scalar.dma_start(out=cols[s][:], in_=share.rearrange("o (p i) -> p (o i)", i=PACK))
-        for t in range(1, PACK):
+        for t in range(1, PACK - 1):
             nc.sync.dma_start(out=planes[t][:], in_=key_rows[:, t, :])
-        for h in range(2):
-            nc.sync.dma_start(out=w_raw[h][:], in_=w_rows[:, :, h * (C // 2) : (h + 1) * (C // 2)])
+        load_w(0)
+        nc.sync.dma_start(out=planes[PACK - 1][:], in_=key_rows[:, PACK - 1, :])
+        load_w(1)
+        load_w(2)
 
         ident = keep.tile([P, P], F32, name="ident")
         make_identity(nc, ident[:])
@@ -56,10 +62,7 @@ def tile_attend_headmerge_pl_kernel(tc, keys, ka, kb, wd, offs, offs2, out_0, ou
             row = keep.tile([P, J], F32, name=f"share{s}")
             dst = row[:].rearrange("m (p i) -> m p i", i=PACK)
             src = spread[:].rearrange("m i p -> m p i")
-            if s == 0:
-                nc.vector.tensor_copy(out=dst, in_=src)
-            else:
-                nc.scalar.copy(out=dst, in_=src)
+            nc.vector.tensor_copy(out=dst, in_=src)
             shares.append(row)
 
         terms = [keep.tile([P, PACK, J], F32, name=f"term{s}") for s in range(2)]
@@ -74,14 +77,14 @@ def tile_attend_headmerge_pl_kernel(tc, keys, ka, kb, wd, offs, offs2, out_0, ou
                     MULT,
                 )
 
-        x_bf = [keep.tile([P, CH, PACK], BF16, name=f"x_bf{c}", align_bytes=64) for c in range(NCH)]
+        x_bf = [keep.tile([P, CH, PACK], BF16, name="x_bf_first", align_bytes=64)[:]]
         x_codes = [keep.tile([P, CH], I32, name=f"x_codes{c}", align_bytes=64) for c in range(NCH)]
         x_scales = [keep.tile([P, CH], U8, name=f"x_scales{c}", align_bytes=64) for c in range(NCH)]
 
         def merge(c):
             js = slice(c * CH, (c + 1) * CH)
             nc.vector.tensor_tensor(
-                x_bf[c][:].rearrange("p (g i) t -> p g t i", i=LINE),
+                x_bf[c].rearrange("p (g i) t -> p g t i", i=LINE),
                 terms[0][:, :, js].rearrange("p t (g i) -> p g t i", i=LINE),
                 terms[1][:, :, js].rearrange("p t (g i) -> p g t i", i=LINE),
                 ADD,
@@ -89,15 +92,15 @@ def tile_attend_headmerge_pl_kernel(tc, keys, ka, kb, wd, offs, offs2, out_0, ou
 
         def quant_x(c):
             nc.vector.quantize_mx(
-                out=x_codes[c][:].bitcast(FP8X4), scales=x_scales[c][:], in_=x_bf[c][:].rearrange("p j t -> p (j t)")
+                out=x_codes[c][:].bitcast(FP8X4), scales=x_scales[c][:], in_=x_bf[c].rearrange("p j t -> p (j t)")
             )
 
-        w_bf = keep.tile([P, PACK, P, PACK], BF16, name="w_bf", align_bytes=64)
+        w_bf = keep.tile([P, PACK, P, PACK], BF16, name="w_bf", tag="staged", align_bytes=64)
         w_codes = keep.tile([P, C], I32, name="w_codes", align_bytes=64)
         w_scales = keep.tile([P, C], U8, name="w_scales", align_bytes=64)
-        for h in range(2):
+        for h, (c0, c1) in enumerate(W_PIECES):
             nc.scalar.copy(
-                out=w_bf[:, :, h * (P // 2) : (h + 1) * (P // 2), :].rearrange("p t m r -> p m r t"),
+                out=w_bf[:, :, c0 // PACK : c1 // PACK, :].rearrange("p t m r -> p m r t"),
                 in_=w_raw[h][:].rearrange("p r (m t) -> p m r t", t=PACK),
             )
 
@@ -106,7 +109,7 @@ def tile_attend_headmerge_pl_kernel(tc, keys, ka, kb, wd, offs, offs2, out_0, ou
                 out=w_codes[:].bitcast(FP8X4), scales=w_scales[:], in_=w_bf[:].rearrange("p t m r -> p (t m r)")
             )
 
-        acc = [psum.tile([P, PACK, CH], F32, name=f"acc{c}") for c in range(NCH)]
+        acc = [psum.tile([P, PACK, CH], F32, name=f"acc{c}") for c in range(NCH - 1)]
         y = [keep.tile([P, PACK, CH], F32, name=f"y{c}") for c in range(NCH)]
         y_bf = [keep.tile([P, CH, PACK], BF16, name=f"y_bf{c}", align_bytes=64) for c in range(NCH)]
         y_codes = keep.tile([P, J], I32, name="y_codes", align_bytes=64)
@@ -131,11 +134,37 @@ def tile_attend_headmerge_pl_kernel(tc, keys, ka, kb, wd, offs, offs2, out_0, ou
             nc.scalar.copy(out=y[c][:], in_=acc[c][:])
             nc.sync.dma_start(out=y_rows[:, :, js], in_=y[c][:])
 
+        def project_last():
+            c = NCH - 1
+            half = PACK // 2
+            banks = [psum.tile([P, half, CH], F32, name=f"acc_last{u}") for u in range(2)]
+            for t in range(PACK):
+                ms = slice(t * P, (t + 1) * P)
+                nc.tensor.matmul_mx(
+                    out=banks[t // half][:, t % half, :],
+                    lhsT=w_codes[:, ms].bitcast(FP8X4),
+                    lhsT_scale=w_scales[:, ms],
+                    rhs=x_codes[c][:].bitcast(FP8X4),
+                    rhs_scale=x_scales[c][:],
+                    start=True,
+                    stop=True,
+                )
+            for u in range(2):
+                v = 1 - u
+                nc.vector.tensor_copy(
+                    out=y_bf[c][:, :, u * half : (u + 1) * half], in_=banks[u][:].rearrange("p t j -> p j t")
+                )
+                nc.scalar.copy(out=y[c][:, v * half : (v + 1) * half, :], in_=banks[v][:])
+            nc.sync.dma_start(out=y_rows[:, :, c * CH :], in_=y[c][:])
+
         def round_y(c):
             nc.vector.tensor_copy(
                 out=y_bf[c][:].rearrange("p (g i) t -> p g t i", i=LINE),
                 in_=y[c][:].rearrange("p t (g i) -> p g t i", i=LINE),
             )
+
+        def round_y_from_psum(c):
+            nc.scalar.copy(out=y_bf[c][:], in_=acc[c][:].rearrange("p t j -> p j t"))
 
         def quant_y(c):
             js = slice(c * CH, (c + 1) * CH)
@@ -151,28 +180,29 @@ def tile_attend_headmerge_pl_kernel(tc, keys, ka, kb, wd, offs, offs2, out_0, ou
         merge(0)
         gather(last, 2 * CH, 3 * CH)
         quant_x(0)
+        quant_w()
+        x_rest = keep.tile([P, NCH - 1, CH, PACK], BF16, name="x_bf_rest", tag="staged", align_bytes=64)
+        x_bf.extend(x_rest[:, c, :, :] for c in range(NCH - 1))
+        project(0)
+        round_y_from_psum(0)
         merge(1)
         gather(last, 3 * CH, 4 * CH)
-        quant_w()
         quant_x(1)
-        project(0)
         project(1)
+        round_y_from_psum(1)
         merge(2)
         merge(3)
         quant_x(2)
         project(2)
-        round_y(0)
         quant_x(3)
-        project(3)
-        round_y(1)
         quant_y(0)
         round_y(2)
         quant_y(1)
-        nc.sync.dma_start(out=word_rows[:, : J // 2], in_=y_codes[:, : J // 2])
-        round_y(3)
         quant_y(2)
+        nc.sync.dma_start(out=word_rows[:, : 3 * CH], in_=y_codes[:, : 3 * CH])
+        project_last()
         quant_y(3)
-        nc.sync.dma_start(out=word_rows[:, J // 2 :], in_=y_codes[:, J // 2 :])
+        nc.sync.dma_start(out=word_rows[:, 3 * CH :], in_=y_codes[:, 3 * CH :])
         for q in range(4):
             queue = nc.scalar if q % 2 else nc.sync
             queue.dma_start(out=scale_rows[4 * q : 4 * q + 4, :], in_=y_scales[32 * q : 32 * q + 4, :].bitcast(I32))

@@ -20,13 +20,15 @@ PACK = 4
 CH = 128
 NCH = J // CH
 LINE = 4
-W_PIECES = ((0, 256), (256, 384), (384, 512))
+TURNED = 2
+W_PIECES = ((0, 128), (128, 256), (256, 384), (384, 512))
 
 
 def tile_attend_headmerge_pl_kernel(tc, keys, ka, kb, wd, offs, offs2, out_0, out_1, out_2):
     nc = tc.nc
     with ExitStack() as ctx:
         keep = ctx.enter_context(tc.tile_pool(name="keep", bufs=1))
+        stage = ctx.enter_context(tc.tile_pool(name="stage", bufs=1))
         psum = ctx.enter_context(tc.psum_pool(name="psum", bufs=1))
 
         list_a = keep.tile([P, J // 16], U16, name="list_a")
@@ -35,35 +37,38 @@ def tile_attend_headmerge_pl_kernel(tc, keys, ka, kb, wd, offs, offs2, out_0, ou
         key_rows = keys.rearrange("(p t) n -> p t n", t=PACK)
         w_rows = wd.rearrange("(p r) c -> p r c", r=PACK)
         w_raw = [keep.tile([P, PACK, c1 - c0], F32, name=f"w_raw{c0}") for c0, c1 in W_PIECES]
-        cols = [keep.tile([P, PACK], F32, name=f"share_cols{s}") for s in range(2)]
+        cols = [keep.tile([P, PACK], F32, name="cols_a")[:], stage.tile([P, 32], F32, name="cols_b", align_bytes=64, offset=C * 8 - 64)[:, :PACK]]
 
         def load_w(h):
             nc.sync.dma_start(out=w_raw[h][:], in_=w_rows[:, :, W_PIECES[h][0] : W_PIECES[h][1]])
 
         for s, share in enumerate((ka, kb)):
-            nc.sync.dma_start(out=cols[s][:], in_=share.rearrange("o (p i) -> p (o i)", i=PACK))
+            nc.sync.dma_start(out=cols[s], in_=share.rearrange("o (p i) -> p (o i)", i=PACK))
         nc.sync.dma_start(out=planes[0][:], in_=key_rows[:, 0, :])
         nc.sync.dma_start(list_a[:], offs)
         nc.sync.dma_start(list_b[:], offs2)
-        for t in range(1, PACK - 1):
+        for t in range(1, PACK):
             nc.sync.dma_start(out=planes[t][:], in_=key_rows[:, t, :])
-        load_w(0)
-        nc.sync.dma_start(out=planes[PACK - 1][:], in_=key_rows[:, PACK - 1, :])
-        load_w(1)
-        load_w(2)
+            load_w(t - 1)
+        load_w(3)
 
         ident = keep.tile([P, P], F32, name="ident")
         make_identity(nc, ident[:])
-        shares = []
+        spread = [psum.tile([P, PACK, P], F32, name=f"spread{s}", tag=f"turn{s}") for s in range(2)]
         for s in range(2):
-            spread = psum.tile([P, PACK, P], F32, name=f"spread{s}")
             for i in range(PACK):
-                nc.tensor.transpose(spread[:, i, :], cols[s][:, i : i + 1].to_broadcast([P, P]), ident[:])
-            row = keep.tile([P, J], F32, name=f"share{s}")
-            dst = row[:].rearrange("m (p i) -> m p i", i=PACK)
-            src = spread[:].rearrange("m i p -> m p i")
-            nc.vector.tensor_copy(out=dst, in_=src)
-            shares.append(row)
+                nc.tensor.transpose(spread[s][:, i, :], cols[s][:, i : i + 1].to_broadcast([P, P]), ident[:])
+        first_share = keep.tile([P, J], F32, name="first_share")
+        shares = [
+            stage.tile([P, J], F32, name="share_a", align_bytes=64, offset=C * 8),
+            keep.tile([P, J], F32, name="share_b"),
+        ]
+        for move, row, s in (
+            (nc.vector.tensor_copy, first_share, 0),
+            (nc.scalar.copy, shares[1], 1),
+            (nc.scalar.copy, shares[0], 0),
+        ):
+            move(out=row[:].rearrange("m (p i) -> m p i", i=PACK), in_=spread[s][:].rearrange("m i p -> m p i"))
 
         terms = [keep.tile([P, PACK, J], F32, name=f"term{s}") for s in range(2)]
         lists = (list_a, list_b)
@@ -73,18 +78,40 @@ def tile_attend_headmerge_pl_kernel(tc, keys, ka, kb, wd, offs, offs2, out_0, ou
                 nc.vector.tensor_tensor(
                     terms[s][:, t, j0:j1],
                     planes[t][:].indirect(lists[s][:, j0 // 16 : j1 // 16]),
-                    shares[s][:, j0:j1],
+                    (first_share if (t, s) == (0, 0) else shares[s])[:, j0:j1],
                     MULT,
                 )
 
-        x_bf = [keep.tile([P, CH, PACK], BF16, name="x_bf_first", align_bytes=64)[:]]
-        x_codes = [keep.tile([P, CH], I32, name=f"x_codes{c}", align_bytes=64) for c in range(NCH)]
+        w_bf = stage.tile([P, PACK, P, PACK], BF16, name="w_bf", align_bytes=64, offset=0)
+        x_bf = [
+            stage.tile([P, CH, PACK], BF16, name=f"x_bf{c}", align_bytes=64, offset=C * 8 + J * 4 + (c % TURNED) * CH * 8)
+            for c in range(NCH)
+        ]
+        x_codes = [
+            stage.tile([P, CH], I32, name=f"x_codes{c}", align_bytes=64, offset=c * CH * 4) for c in range(TURNED)
+        ]
+        x_codes.extend(keep.tile([P, CH], I32, name=f"x_codes{c}", align_bytes=64) for c in range(TURNED, NCH))
         x_scales = [keep.tile([P, CH], U8, name=f"x_scales{c}", align_bytes=64) for c in range(NCH)]
+        back = [psum.tile([P, 2, CH], F32, name=f"back{c}") for c in range(TURNED)]
+
+        def sum_turned(dst, t, c):
+            for s in range(2):
+                nc.tensor.matmul(
+                    dst, lhsT=terms[s][:, t, c * CH : (c + 1) * CH], rhs=ident[:],
+                    is_transpose=True, start=(s == 0), stop=(s == 1),
+                )
+
+        def turn_back(c, u, pairs):
+            nc.tensor.transpose(back[c][:, u, :], pairs.rearrange("j p e -> j (p e)").bitcast(F32), ident[:])
+
+        def weave(c):
+            words = x_bf[c][:].rearrange("p j t -> p (j t)").bitcast(F32).rearrange("p (j u) -> p j u", u=2)
+            nc.scalar.copy(out=words, in_=back[c][:].rearrange("p u j -> p j u"))
 
         def merge(c):
             js = slice(c * CH, (c + 1) * CH)
             nc.vector.tensor_tensor(
-                x_bf[c].rearrange("p (g i) t -> p g t i", i=LINE),
+                x_bf[c][:].rearrange("p (g i) t -> p g t i", i=LINE),
                 terms[0][:, :, js].rearrange("p t (g i) -> p g t i", i=LINE),
                 terms[1][:, :, js].rearrange("p t (g i) -> p g t i", i=LINE),
                 ADD,
@@ -92,13 +119,14 @@ def tile_attend_headmerge_pl_kernel(tc, keys, ka, kb, wd, offs, offs2, out_0, ou
 
         def quant_x(c):
             nc.vector.quantize_mx(
-                out=x_codes[c][:].bitcast(FP8X4), scales=x_scales[c][:], in_=x_bf[c].rearrange("p j t -> p (j t)")
+                out=x_codes[c][:].bitcast(FP8X4), scales=x_scales[c][:], in_=x_bf[c][:].rearrange("p j t -> p (j t)")
             )
 
-        w_bf = keep.tile([P, PACK, P, PACK], BF16, name="w_bf", tag="staged", align_bytes=64)
         w_codes = keep.tile([P, C], I32, name="w_codes", align_bytes=64)
         w_scales = keep.tile([P, C], U8, name="w_scales", align_bytes=64)
-        for h, (c0, c1) in enumerate(W_PIECES):
+
+        def deal_w(h):
+            c0, c1 = W_PIECES[h]
             nc.scalar.copy(
                 out=w_bf[:, :, c0 // PACK : c1 // PACK, :].rearrange("p t m r -> p m r t"),
                 in_=w_raw[h][:].rearrange("p r (m t) -> p m r t", t=PACK),
@@ -109,7 +137,7 @@ def tile_attend_headmerge_pl_kernel(tc, keys, ka, kb, wd, offs, offs2, out_0, ou
                 out=w_codes[:].bitcast(FP8X4), scales=w_scales[:], in_=w_bf[:].rearrange("p t m r -> p (t m r)")
             )
 
-        acc = [psum.tile([P, PACK, CH], F32, name=f"acc{c}") for c in range(NCH - 1)]
+        acc = [psum.tile([P, PACK, CH], F32, name=f"acc{c}") for c in range(NCH)]
         y = [keep.tile([P, PACK, CH], F32, name=f"y{c}") for c in range(NCH)]
         y_bf = [keep.tile([P, CH, PACK], BF16, name=f"y_bf{c}", align_bytes=64) for c in range(NCH)]
         y_codes = keep.tile([P, J], I32, name="y_codes", align_bytes=64)
@@ -134,37 +162,11 @@ def tile_attend_headmerge_pl_kernel(tc, keys, ka, kb, wd, offs, offs2, out_0, ou
             nc.scalar.copy(out=y[c][:], in_=acc[c][:])
             nc.sync.dma_start(out=y_rows[:, :, js], in_=y[c][:])
 
-        def project_last():
-            c = NCH - 1
-            half = PACK // 2
-            banks = [psum.tile([P, half, CH], F32, name=f"acc_last{u}") for u in range(2)]
-            for t in range(PACK):
-                ms = slice(t * P, (t + 1) * P)
-                nc.tensor.matmul_mx(
-                    out=banks[t // half][:, t % half, :],
-                    lhsT=w_codes[:, ms].bitcast(FP8X4),
-                    lhsT_scale=w_scales[:, ms],
-                    rhs=x_codes[c][:].bitcast(FP8X4),
-                    rhs_scale=x_scales[c][:],
-                    start=True,
-                    stop=True,
-                )
-            for u in range(2):
-                v = 1 - u
-                nc.vector.tensor_copy(
-                    out=y_bf[c][:, :, u * half : (u + 1) * half], in_=banks[u][:].rearrange("p t j -> p j t")
-                )
-                nc.scalar.copy(out=y[c][:, v * half : (v + 1) * half, :], in_=banks[v][:])
-            nc.sync.dma_start(out=y_rows[:, :, c * CH :], in_=y[c][:])
-
         def round_y(c):
             nc.vector.tensor_copy(
                 out=y_bf[c][:].rearrange("p (g i) t -> p g t i", i=LINE),
                 in_=y[c][:].rearrange("p t (g i) -> p g t i", i=LINE),
             )
-
-        def round_y_from_psum(c):
-            nc.scalar.copy(out=y_bf[c][:], in_=acc[c][:].rearrange("p t j -> p j t"))
 
         def quant_y(c):
             js = slice(c * CH, (c + 1) * CH)
@@ -172,35 +174,50 @@ def tile_attend_headmerge_pl_kernel(tc, keys, ka, kb, wd, offs, offs2, out_0, ou
                 out=y_codes[:, js].bitcast(FP8X4), scales=y_scales[:, js], in_=y_bf[c][:].rearrange("p j t -> p (j t)")
             )
 
-        for t in range(PACK - 1):
+        early = psum.tile([P, TURNED, 2, P], F32, name="early", tag="turn0")
+        for t in range(2):
             gather(t, 0, J)
-        last = PACK - 1
-        gather(last, 0, CH)
-        gather(last, CH, 2 * CH)
-        merge(0)
-        gather(last, 2 * CH, 3 * CH)
-        quant_x(0)
+            for c in range(TURNED):
+                sum_turned(early[:, c, t, :], t, c)
+        deal_w(0)
+        deal_w(1)
+        early_pairs = w_bf[:, :TURNED, P // 2 :, :].rearrange("j c m (q e) -> j c (m q) e", e=2)
+        nc.scalar.copy(out=early_pairs, in_=early[:].rearrange("j c e p -> j c p e"))
+        for c in range(TURNED):
+            turn_back(c, 0, early_pairs[:, c, :, :])
+        deal_w(2)
+        deal_w(3)
+        late = [psum.tile([P, 2, P], F32, name=f"late{c}", tag=f"turn{1 - c}") for c in range(TURNED)]
+        gather(2, 0, J)
+        for c in range(TURNED):
+            sum_turned(late[c][:, 0, :], 2, c)
+        for c in range(TURNED):
+            gather(3, c * CH, (c + 1) * CH)
+            sum_turned(late[c][:, 1, :], 3, c)
+            pairs = keep.tile([P, P, 2], BF16, name=f"late_pairs{c}")
+            nc.scalar.copy(out=pairs[:], in_=late[c][:].rearrange("j e p -> j p e"))
+            turn_back(c, 1, pairs[:])
+            weave(c)
+        gather(3, TURNED * CH, J)
         quant_w()
-        x_rest = keep.tile([P, NCH - 1, CH, PACK], BF16, name="x_bf_rest", tag="staged", align_bytes=64)
-        x_bf.extend(x_rest[:, c, :, :] for c in range(NCH - 1))
+        quant_x(0)
         project(0)
-        round_y_from_psum(0)
-        merge(1)
-        gather(last, 3 * CH, 4 * CH)
+        merge(2)
         quant_x(1)
         project(1)
-        round_y_from_psum(1)
-        merge(2)
         merge(3)
         quant_x(2)
         project(2)
         quant_x(3)
+        project(3)
+        round_y(0)
+        round_y(1)
         quant_y(0)
-        round_y(2)
         quant_y(1)
+        round_y(2)
         quant_y(2)
         nc.sync.dma_start(out=word_rows[:, : 3 * CH], in_=y_codes[:, : 3 * CH])
-        project_last()
+        round_y(3)
         quant_y(3)
         nc.sync.dma_start(out=word_rows[:, 3 * CH :], in_=y_codes[:, 3 * CH :])
         for q in range(4):

@@ -14,14 +14,15 @@ U8 = mybir.dt.uint8
 FP8X4 = mybir.dt.float8_e4m3fn_x4
 MULT = mybir.AluOpType.mult
 ADD = mybir.AluOpType.add
+COPY = mybir.ActivationFunctionType.Copy
 
 P = 128
 PACK = 4
 CH = 128
 NCH = J // CH
 LINE = 4
-TURNED = 2
-W_PIECES = ((0, 128), (128, 256), (256, 384), (384, 512))
+HALF = J // 2
+ON_SCALAR = 1
 
 
 def tile_attend_headmerge_pl_kernel(tc, keys, ka, kb, wd, offs, offs2, out_0, out_1, out_2):
@@ -36,11 +37,16 @@ def tile_attend_headmerge_pl_kernel(tc, keys, ka, kb, wd, offs, offs2, out_0, ou
         planes = [keep.tile([P, T], F32, name=f"plane{t}") for t in range(PACK)]
         key_rows = keys.rearrange("(p t) n -> p t n", t=PACK)
         w_rows = wd.rearrange("(p r) c -> p r c", r=PACK)
-        w_raw = [keep.tile([P, PACK, c1 - c0], F32, name=f"w_raw{c0}") for c0, c1 in W_PIECES]
-        cols = [keep.tile([P, PACK], F32, name="cols_a")[:], stage.tile([P, 32], F32, name="cols_b", align_bytes=64, offset=C * 8 - 64)[:, :PACK]]
-
-        def load_w(h):
-            nc.sync.dma_start(out=w_raw[h][:], in_=w_rows[:, :, W_PIECES[h][0] : W_PIECES[h][1]])
+        w_raw = [
+            stage.tile([P, PACK, C // 2], F32, name="w_raw0", align_bytes=64, offset=J * 4 + C * 8),
+            keep.tile([P, PACK, C // 2], F32, name="w_raw1"),
+        ]
+        term_a = keep.tile([P, PACK, J], F32, name="term_a")
+        term_b = keep.tile([P, PACK, J], F32, name="term_b")
+        raw_early = keep.tile([P, 2 * J], F32, name="raw_early")
+        raw_last = stage.tile([P, J], F32, name="raw_last", align_bytes=64, offset=0)
+        raw = [None, raw_early[:, :J], raw_early[:, J:], raw_last[:]]
+        cols = [keep.tile([P, PACK], F32, name="cols_a")[:], raw_early[:, J - 2 : J + 2]]
 
         for s, share in enumerate((ka, kb)):
             nc.sync.dma_start(out=cols[s], in_=share.rearrange("o (p i) -> p (o i)", i=PACK))
@@ -49,8 +55,8 @@ def tile_attend_headmerge_pl_kernel(tc, keys, ka, kb, wd, offs, offs2, out_0, ou
         nc.sync.dma_start(list_b[:], offs2)
         for t in range(1, PACK):
             nc.sync.dma_start(out=planes[t][:], in_=key_rows[:, t, :])
-            load_w(t - 1)
-        load_w(3)
+        for h in range(2):
+            nc.sync.dma_start(out=w_raw[h][:], in_=w_rows[:, :, h * C // 2 : (h + 1) * C // 2])
 
         ident = keep.tile([P, P], F32, name="ident")
         make_identity(nc, ident[:])
@@ -58,167 +64,176 @@ def tile_attend_headmerge_pl_kernel(tc, keys, ka, kb, wd, offs, offs2, out_0, ou
         for s in range(2):
             for i in range(PACK):
                 nc.tensor.transpose(spread[s][:, i, :], cols[s][:, i : i + 1].to_broadcast([P, P]), ident[:])
-        first_share = keep.tile([P, J], F32, name="first_share")
-        shares = [
-            stage.tile([P, J], F32, name="share_a", align_bytes=64, offset=C * 8),
-            keep.tile([P, J], F32, name="share_b"),
-        ]
-        for move, row, s in (
-            (nc.vector.tensor_copy, first_share, 0),
-            (nc.scalar.copy, shares[1], 1),
-            (nc.scalar.copy, shares[0], 0),
-        ):
-            move(out=row[:].rearrange("m (p i) -> m p i", i=PACK), in_=spread[s][:].rearrange("m i p -> m p i"))
+        shares = [keep.tile([P, J], F32, name=f"share{s}") for s in range(2)]
+        for s, move in enumerate((nc.scalar.copy, nc.vector.tensor_copy)):
+            move(out=shares[s][:].rearrange("m (p i) -> m p i", i=PACK), in_=spread[s][:].rearrange("m i p -> m p i"))
 
-        terms = [keep.tile([P, PACK, J], F32, name=f"term{s}") for s in range(2)]
-        lists = (list_a, list_b)
+        def gather_a(t):
+            nc.vector.tensor_tensor(term_a[:, t, :], planes[t][:].indirect(list_a[:]), shares[0][:], MULT)
 
-        def gather(t, j0, j1):
-            for s in range(2):
-                nc.vector.tensor_tensor(
-                    terms[s][:, t, j0:j1],
-                    planes[t][:].indirect(lists[s][:, j0 // 16 : j1 // 16]),
-                    (first_share if (t, s) == (0, 0) else shares[s])[:, j0:j1],
-                    MULT,
-                )
+        def gather_b(t):
+            if t < ON_SCALAR:
+                nc.vector.tensor_tensor(term_b[:, t, :], planes[t][:].indirect(list_b[:]), shares[1][:], MULT)
+            else:
+                nc.scalar.activation(raw[t], planes[t][:].indirect(list_b[:]), COPY)
 
-        w_bf = stage.tile([P, PACK, P, PACK], BF16, name="w_bf", align_bytes=64, offset=0)
-        x_bf = [
-            stage.tile([P, CH, PACK], BF16, name=f"x_bf{c}", align_bytes=64, offset=C * 8 + J * 4 + (c % TURNED) * CH * 8)
-            for c in range(NCH)
-        ]
-        x_codes = [
-            stage.tile([P, CH], I32, name=f"x_codes{c}", align_bytes=64, offset=c * CH * 4) for c in range(TURNED)
-        ]
-        x_codes.extend(keep.tile([P, CH], I32, name=f"x_codes{c}", align_bytes=64) for c in range(TURNED, NCH))
-        x_scales = [keep.tile([P, CH], U8, name=f"x_scales{c}", align_bytes=64) for c in range(NCH)]
-        back = [psum.tile([P, 2, CH], F32, name=f"back{c}") for c in range(TURNED)]
+        def scale_b(t, j0, j1):
+            nc.vector.tensor_tensor(term_b[:, t, j0:j1], raw[t][:, j0:j1], shares[1][:, j0:j1], MULT)
 
-        def sum_turned(dst, t, c):
-            for s in range(2):
+        spans = ((0, HALF), (HALF, HALF + CH), (HALF + CH, J))
+        x_bf = [keep.tile([P, HALF, PACK], BF16, name="x_bf_first", align_bytes=64)]
+        x_bf.append(keep.tile([P, CH, PACK], BF16, name="x_bf_turned", align_bytes=64))
+        x_bf.append(stage.tile([P, CH, PACK], BF16, name="x_bf_last", align_bytes=64, offset=J * 4))
+        turned = slice(HALF, HALF + CH)
+        back = psum.tile([P, 2, CH], F32, name="back")
+
+        def sum_turned(dst, t):
+            for s, term in enumerate((term_a, term_b)):
                 nc.tensor.matmul(
-                    dst, lhsT=terms[s][:, t, c * CH : (c + 1) * CH], rhs=ident[:],
-                    is_transpose=True, start=(s == 0), stop=(s == 1),
+                    dst, lhsT=term[:, t, turned], rhs=ident[:], is_transpose=True, start=(s == 0), stop=(s == 1)
                 )
 
-        def turn_back(c, u, pairs):
-            nc.tensor.transpose(back[c][:, u, :], pairs.rearrange("j p e -> j (p e)").bitcast(F32), ident[:])
+        def pair_back(u, bank, pairs):
+            nc.scalar.copy(out=pairs[:], in_=bank[:].rearrange("j e p -> j p e"))
+            nc.tensor.transpose(back[:, u, :], pairs[:].rearrange("j p e -> j (p e)").bitcast(F32), ident[:])
 
-        def weave(c):
-            words = x_bf[c][:].rearrange("p j t -> p (j t)").bitcast(F32).rearrange("p (j u) -> p j u", u=2)
-            nc.scalar.copy(out=words, in_=back[c][:].rearrange("p u j -> p j u"))
+        def weave():
+            words = x_bf[1][:].rearrange("p j t -> p (j t)").bitcast(F32).rearrange("p (j u) -> p j u", u=2)
+            nc.scalar.copy(out=words, in_=back[:].rearrange("p u j -> p j u"))
+        x_codes = [keep.tile([P, j1 - j0], I32, name=f"x_codes{j0}", align_bytes=64) for j0, j1 in spans]
+        x_scales = [keep.tile([P, j1 - j0], U8, name=f"x_scales{j0}", align_bytes=64) for j0, j1 in spans]
 
         def merge(c):
             js = slice(c * CH, (c + 1) * CH)
+            dst = x_bf[0][:, js, :] if c < 2 else x_bf[c - 1][:]
             nc.vector.tensor_tensor(
-                x_bf[c][:].rearrange("p (g i) t -> p g t i", i=LINE),
-                terms[0][:, :, js].rearrange("p t (g i) -> p g t i", i=LINE),
-                terms[1][:, :, js].rearrange("p t (g i) -> p g t i", i=LINE),
+                dst.rearrange("p (g i) t -> p g t i", i=LINE),
+                term_a[:, :, js].rearrange("p t (g i) -> p g t i", i=LINE),
+                term_b[:, :, js].rearrange("p t (g i) -> p g t i", i=LINE),
                 ADD,
             )
 
         def quant_x(c):
+            k = max(c - 1, 0)
+            js = slice(c * CH, (c + 1) * CH) if c < 2 else slice(0, CH)
             nc.vector.quantize_mx(
-                out=x_codes[c][:].bitcast(FP8X4), scales=x_scales[c][:], in_=x_bf[c][:].rearrange("p j t -> p (j t)")
+                out=x_codes[k][:, js].bitcast(FP8X4),
+                scales=x_scales[k][:, js],
+                in_=x_bf[k][:, js, :].rearrange("p j t -> p (j t)"),
             )
 
-        w_codes = keep.tile([P, C], I32, name="w_codes", align_bytes=64)
-        w_scales = keep.tile([P, C], U8, name="w_scales", align_bytes=64)
+        w_bf = stage.tile([P, PACK, P, PACK], BF16, name="w_bf", align_bytes=64, offset=J * 4)
+        w_codes = [
+            stage.tile([P, 2 * P], I32, name=f"w_codes{u}", align_bytes=64, offset=u * 2 * P * 4) for u in range(2)
+        ]
+        w_scales = [keep.tile([P, 2 * P], U8, name=f"w_scales{u}", align_bytes=64) for u in range(2)]
 
-        def deal_w(h):
-            c0, c1 = W_PIECES[h]
+        def deal_w(h, t0, t1):
             nc.scalar.copy(
-                out=w_bf[:, :, c0 // PACK : c1 // PACK, :].rearrange("p t m r -> p m r t"),
-                in_=w_raw[h][:].rearrange("p r (m t) -> p m r t", t=PACK),
+                out=w_bf[:, t0:t1, h * P // 2 : (h + 1) * P // 2, :].rearrange("p t m r -> p m r t"),
+                in_=w_raw[h][:].rearrange("p r (m t) -> p m r t", t=PACK)[:, :, :, t0:t1],
             )
 
-        def quant_w():
+        def quant_w(u):
             nc.vector.quantize_mx(
-                out=w_codes[:].bitcast(FP8X4), scales=w_scales[:], in_=w_bf[:].rearrange("p t m r -> p (t m r)")
+                out=w_codes[u][:].bitcast(FP8X4),
+                scales=w_scales[u][:],
+                in_=w_bf[:, 2 * u : 2 * u + 2, :, :].rearrange("p t m r -> p (t m r)"),
             )
 
-        acc = [psum.tile([P, PACK, CH], F32, name=f"acc{c}") for c in range(NCH)]
-        y = [keep.tile([P, PACK, CH], F32, name=f"y{c}") for c in range(NCH)]
-        y_bf = [keep.tile([P, CH, PACK], BF16, name=f"y_bf{c}", align_bytes=64) for c in range(NCH)]
+        y_first = keep.tile([P, PACK, HALF], F32, name="y_first")
+        y_late = [keep.tile([P, PACK, CH], F32, name=f"y_late{k}") for k in range(2)]
+        y = [y_first[:, :, :CH], y_first[:, :, CH:], y_late[0][:], y_late[1][:]]
+        y_bf = [keep.tile([P, j1 - j0, PACK], BF16, name=f"y_bf{j0}", align_bytes=64) for j0, j1 in spans]
         y_codes = keep.tile([P, J], I32, name="y_codes", align_bytes=64)
         y_scales = keep.tile([P, J], U8, name="y_scales", align_bytes=64)
         y_rows = out_0.rearrange("(p t) j -> p t j", t=PACK)
         word_rows = out_1[0].rearrange("l c r -> l (c r)").bitcast(I32)
         scale_rows = out_2[0].bitcast(I32)
 
-        def project(c):
-            js = slice(c * CH, (c + 1) * CH)
+        def product(dst, t, k):
+            ms = slice(t % 2 * P, (t % 2 + 1) * P)
+            nc.tensor.matmul_mx(
+                out=dst,
+                lhsT=w_codes[t // 2][:, ms].bitcast(FP8X4),
+                lhsT_scale=w_scales[t // 2][:, ms],
+                rhs=x_codes[k][:].bitcast(FP8X4),
+                rhs_scale=x_scales[k][:],
+                start=True,
+                stop=True,
+            )
+
+        def project_first(u):
+            acc = psum.tile([P, 2, HALF], F32, name=f"acc_first{u}")
+            for e in range(2):
+                product(acc[:, e, :], 2 * u + e, 0)
+            nc.scalar.copy(out=y_first[:, 2 * u : 2 * u + 2, :], in_=acc[:])
+            nc.sync.dma_start(out=y_rows[:, 2 * u : 2 * u + 2, :HALF], in_=y_first[:, 2 * u : 2 * u + 2, :])
+
+        def project_late(k):
+            acc = psum.tile([P, PACK, CH], F32, name=f"acc_late{k}")
             for t in range(PACK):
-                ms = slice(t * P, (t + 1) * P)
-                nc.tensor.matmul_mx(
-                    out=acc[c][:, t, :],
-                    lhsT=w_codes[:, ms].bitcast(FP8X4),
-                    lhsT_scale=w_scales[:, ms],
-                    rhs=x_codes[c][:].bitcast(FP8X4),
-                    rhs_scale=x_scales[c][:],
-                    start=True,
-                    stop=True,
-                )
-            nc.scalar.copy(out=y[c][:], in_=acc[c][:])
-            nc.sync.dma_start(out=y_rows[:, :, js], in_=y[c][:])
+                product(acc[:, t, :], t, k)
+            nc.scalar.copy(out=y_late[k - 1][:], in_=acc[:])
+            nc.sync.dma_start(out=y_rows[:, :, spans[k][0] : spans[k][1]], in_=y_late[k - 1][:])
+            if k == 2:
+                nc.scalar.copy(out=y_bf[k][:], in_=acc[:].rearrange("p t j -> p j t"))
 
         def round_y(c):
+            dst = y_bf[0][:, c * CH : (c + 1) * CH, :] if c < 2 else y_bf[c - 1][:]
             nc.vector.tensor_copy(
-                out=y_bf[c][:].rearrange("p (g i) t -> p g t i", i=LINE),
-                in_=y[c][:].rearrange("p t (g i) -> p g t i", i=LINE),
+                out=dst.rearrange("p (g i) t -> p g t i", i=LINE),
+                in_=y[c].rearrange("p t (g i) -> p g t i", i=LINE),
             )
 
-        def quant_y(c):
-            js = slice(c * CH, (c + 1) * CH)
+        def quant_y(k):
+            js = slice(spans[k][0], spans[k][1])
             nc.vector.quantize_mx(
-                out=y_codes[:, js].bitcast(FP8X4), scales=y_scales[:, js], in_=y_bf[c][:].rearrange("p j t -> p (j t)")
+                out=y_codes[:, js].bitcast(FP8X4), scales=y_scales[:, js], in_=y_bf[k][:].rearrange("p j t -> p (j t)")
             )
 
-        early = psum.tile([P, TURNED, 2, P], F32, name="early", tag="turn0")
-        for t in range(2):
-            gather(t, 0, J)
-            for c in range(TURNED):
-                sum_turned(early[:, c, t, :], t, c)
-        deal_w(0)
-        deal_w(1)
-        early_pairs = w_bf[:, :TURNED, P // 2 :, :].rearrange("j c m (q e) -> j c (m q) e", e=2)
-        nc.scalar.copy(out=early_pairs, in_=early[:].rearrange("j c e p -> j c p e"))
-        for c in range(TURNED):
-            turn_back(c, 0, early_pairs[:, c, :, :])
-        deal_w(2)
-        deal_w(3)
-        late = [psum.tile([P, 2, P], F32, name=f"late{c}", tag=f"turn{1 - c}") for c in range(TURNED)]
-        gather(2, 0, J)
-        for c in range(TURNED):
-            sum_turned(late[c][:, 0, :], 2, c)
-        for c in range(TURNED):
-            gather(3, c * CH, (c + 1) * CH)
-            sum_turned(late[c][:, 1, :], 3, c)
-            pairs = keep.tile([P, P, 2], BF16, name=f"late_pairs{c}")
-            nc.scalar.copy(out=pairs[:], in_=late[c][:].rearrange("j e p -> j p e"))
-            turn_back(c, 1, pairs[:])
-            weave(c)
-        gather(3, TURNED * CH, J)
-        quant_w()
+        sums = [psum.tile([P, 2, P], F32, name=f"sums{u}", tag=f"turn{u}") for u in range(2)]
+        pairs = [
+            keep.tile([P, P, 2], BF16, name="pairs0"),
+            stage.tile([P, P, 2], BF16, name="pairs1", align_bytes=64, offset=J * 4 + C * 8),
+        ]
+        for t in range(PACK):
+            gather_a(t)
+            gather_b(t)
+            if t == 2:
+                pair_back(0, sums[0], pairs[0])
+            if ON_SCALAR <= t < PACK - 1:
+                scale_b(t, 0, J)
+            if t < PACK - 1:
+                sum_turned(sums[t // 2][:, t % 2, :], t)
+        scale_b(PACK - 1, 0, HALF)
+        scale_b(PACK - 1, HALF, J)
+        sum_turned(sums[1][:, 1, :], PACK - 1)
+        deal_w(0, 0, PACK)
+        pair_back(1, sums[1], pairs[1])
+        deal_w(1, 0, 2)
+        deal_w(1, 2, PACK)
+        weave()
+        merge(0)
+        merge(1)
         quant_x(0)
-        project(0)
-        merge(2)
         quant_x(1)
-        project(1)
+        quant_w(0)
+        project_first(0)
+        quant_w(1)
+        project_first(1)
         merge(3)
         quant_x(2)
-        project(2)
+        project_late(1)
         quant_x(3)
-        project(3)
+        project_late(2)
         round_y(0)
         round_y(1)
+        round_y(2)
         quant_y(0)
         quant_y(1)
-        round_y(2)
-        quant_y(2)
         nc.sync.dma_start(out=word_rows[:, : 3 * CH], in_=y_codes[:, : 3 * CH])
-        round_y(3)
-        quant_y(3)
+        quant_y(2)
         nc.sync.dma_start(out=word_rows[:, 3 * CH :], in_=y_codes[:, 3 * CH :])
         for q in range(4):
             queue = nc.scalar if q % 2 else nc.sync

@@ -22,7 +22,8 @@ CH = 128
 NCH = J // CH
 LINE = 4
 HALF = J // 2
-ON_SCALAR = 1
+ON_SCALAR = 0
+LEAD = T // 4
 
 
 def tile_attend_headmerge_pl_kernel(tc, keys, ka, kb, wd, offs, offs2, out_0, out_1, out_2):
@@ -43,16 +44,17 @@ def tile_attend_headmerge_pl_kernel(tc, keys, ka, kb, wd, offs, offs2, out_0, ou
         ]
         term_a = keep.tile([P, PACK, J], F32, name="term_a")
         term_b = keep.tile([P, PACK, J], F32, name="term_b")
-        raw_early = keep.tile([P, 2 * J], F32, name="raw_early")
+        raw_early = keep.tile([P, 3 * J], F32, name="raw_early")
         raw_last = stage.tile([P, J], F32, name="raw_last", align_bytes=64, offset=0)
-        raw = [None, raw_early[:, :J], raw_early[:, J:], raw_last[:]]
+        raw = [raw_early[:, :J], raw_early[:, J : 2 * J], raw_early[:, 2 * J :], raw_last[:]]
         cols = [keep.tile([P, PACK], F32, name="cols_a")[:], raw_early[:, J - 2 : J + 2]]
 
+        nc.sync.dma_start(out=planes[0][:, :LEAD], in_=key_rows[:, 0, :LEAD])
         for s, share in enumerate((ka, kb)):
             nc.sync.dma_start(out=cols[s], in_=share.rearrange("o (p i) -> p (o i)", i=PACK))
-        nc.sync.dma_start(out=planes[0][:], in_=key_rows[:, 0, :])
         nc.sync.dma_start(list_a[:], offs)
         nc.sync.dma_start(list_b[:], offs2)
+        nc.sync.dma_start(out=planes[0][:, LEAD:], in_=key_rows[:, 0, LEAD:])
         for t in range(1, PACK):
             nc.sync.dma_start(out=planes[t][:], in_=key_rows[:, t, :])
         for h in range(2):
@@ -80,10 +82,11 @@ def tile_attend_headmerge_pl_kernel(tc, keys, ka, kb, wd, offs, offs2, out_0, ou
         def scale_b(t, j0, j1):
             nc.vector.tensor_tensor(term_b[:, t, j0:j1], raw[t][:, j0:j1], shares[1][:, j0:j1], MULT)
 
-        spans = ((0, HALF), (HALF, HALF + CH), (HALF + CH, J))
+        spans = ((0, HALF), (HALF, J))
         x_bf = [keep.tile([P, HALF, PACK], BF16, name="x_bf_first", align_bytes=64)]
         x_bf.append(keep.tile([P, CH, PACK], BF16, name="x_bf_turned", align_bytes=64))
-        x_bf.append(stage.tile([P, CH, PACK], BF16, name="x_bf_last", align_bytes=64, offset=J * 4))
+        w_bf = keep.tile([P, PACK, P, PACK], BF16, name="w_bf", align_bytes=64)
+        x_last = [w_bf[:, 2 * h, : CH // 2, :] for h in range(2)]
         turned = slice(HALF, HALF + CH)
         back = psum.tile([P, 2, CH], F32, name="back")
 
@@ -103,26 +106,21 @@ def tile_attend_headmerge_pl_kernel(tc, keys, ka, kb, wd, offs, offs2, out_0, ou
         x_codes = [keep.tile([P, j1 - j0], I32, name=f"x_codes{j0}", align_bytes=64) for j0, j1 in spans]
         x_scales = [keep.tile([P, j1 - j0], U8, name=f"x_scales{j0}", align_bytes=64) for j0, j1 in spans]
 
-        def merge(c):
-            js = slice(c * CH, (c + 1) * CH)
-            dst = x_bf[0][:, js, :] if c < 2 else x_bf[c - 1][:]
+        def merge(dst, j0, j1):
             nc.vector.tensor_tensor(
                 dst.rearrange("p (g i) t -> p g t i", i=LINE),
-                term_a[:, :, js].rearrange("p t (g i) -> p g t i", i=LINE),
-                term_b[:, :, js].rearrange("p t (g i) -> p g t i", i=LINE),
+                term_a[:, :, j0:j1].rearrange("p t (g i) -> p g t i", i=LINE),
+                term_b[:, :, j0:j1].rearrange("p t (g i) -> p g t i", i=LINE),
                 ADD,
             )
 
-        def quant_x(c):
-            k = max(c - 1, 0)
-            js = slice(c * CH, (c + 1) * CH) if c < 2 else slice(0, CH)
+        def quant_x(k, j0, j1, src):
             nc.vector.quantize_mx(
-                out=x_codes[k][:, js].bitcast(FP8X4),
-                scales=x_scales[k][:, js],
-                in_=x_bf[k][:, js, :].rearrange("p j t -> p (j t)"),
+                out=x_codes[k][:, j0:j1].bitcast(FP8X4),
+                scales=x_scales[k][:, j0:j1],
+                in_=src.rearrange("p j t -> p (j t)"),
             )
 
-        w_bf = stage.tile([P, PACK, P, PACK], BF16, name="w_bf", align_bytes=64, offset=J * 4)
         w_codes = [
             stage.tile([P, 2 * P], I32, name=f"w_codes{u}", align_bytes=64, offset=u * 2 * P * 4) for u in range(2)
         ]
@@ -134,16 +132,16 @@ def tile_attend_headmerge_pl_kernel(tc, keys, ka, kb, wd, offs, offs2, out_0, ou
                 in_=w_raw[h][:].rearrange("p r (m t) -> p m r t", t=PACK)[:, :, :, t0:t1],
             )
 
-        def quant_w(u):
+        def quant_w(t0, t1):
+            ms = slice(t0 % 2 * P, ((t1 - 1) % 2 + 1) * P)
             nc.vector.quantize_mx(
-                out=w_codes[u][:].bitcast(FP8X4),
-                scales=w_scales[u][:],
-                in_=w_bf[:, 2 * u : 2 * u + 2, :, :].rearrange("p t m r -> p (t m r)"),
+                out=w_codes[t0 // 2][:, ms].bitcast(FP8X4),
+                scales=w_scales[t0 // 2][:, ms],
+                in_=w_bf[:, t0:t1, :, :].rearrange("p t m r -> p (t m r)"),
             )
 
         y_first = keep.tile([P, PACK, HALF], F32, name="y_first")
-        y_late = [keep.tile([P, PACK, CH], F32, name=f"y_late{k}") for k in range(2)]
-        y = [y_first[:, :, :CH], y_first[:, :, CH:], y_late[0][:], y_late[1][:]]
+        y_late = keep.tile([P, PACK, HALF], F32, name="y_late")
         y_bf = [keep.tile([P, j1 - j0, PACK], BF16, name=f"y_bf{j0}", align_bytes=64) for j0, j1 in spans]
         y_codes = keep.tile([P, J], I32, name="y_codes", align_bytes=64)
         y_scales = keep.tile([P, J], U8, name="y_scales", align_bytes=64)
@@ -163,33 +161,32 @@ def tile_attend_headmerge_pl_kernel(tc, keys, ka, kb, wd, offs, offs2, out_0, ou
                 stop=True,
             )
 
-        def project_first(u):
-            acc = psum.tile([P, 2, HALF], F32, name=f"acc_first{u}")
-            for e in range(2):
-                product(acc[:, e, :], 2 * u + e, 0)
-            nc.scalar.copy(out=y_first[:, 2 * u : 2 * u + 2, :], in_=acc[:])
-            nc.sync.dma_start(out=y_rows[:, 2 * u : 2 * u + 2, :HALF], in_=y_first[:, 2 * u : 2 * u + 2, :])
+        def project_first(t0, t1):
+            acc = psum.tile([P, t1 - t0, HALF], F32, name=f"acc_first{t0}", tag="turn0" if t0 == 0 else f"acc_first{t0}")
+            for t in range(t0, t1):
+                product(acc[:, t - t0, :], t, 0)
+            nc.scalar.copy(out=y_first[:, t0:t1, :], in_=acc[:])
+            nc.sync.dma_start(out=y_rows[:, t0:t1, :HALF], in_=y_first[:, t0:t1, :])
 
-        def project_late(k):
-            acc = psum.tile([P, PACK, CH], F32, name=f"acc_late{k}")
-            for t in range(PACK):
-                product(acc[:, t, :], t, k)
-            nc.scalar.copy(out=y_late[k - 1][:], in_=acc[:])
-            nc.sync.dma_start(out=y_rows[:, :, spans[k][0] : spans[k][1]], in_=y_late[k - 1][:])
-            if k == 2:
-                nc.scalar.copy(out=y_bf[k][:], in_=acc[:].rearrange("p t j -> p j t"))
+        def project_late(t0, t1, move, tag):
+            acc = psum.tile([P, t1 - t0, HALF], F32, name=f"acc_late{t0}", tag=tag)
+            for t in range(t0, t1):
+                product(acc[:, t - t0, :], t, 1)
+            move(out=y_late[:, t0:t1, :], in_=acc[:])
+            nc.sync.dma_start(out=y_rows[:, t0:t1, HALF:], in_=y_late[:, t0:t1, :])
 
-        def round_y(c):
-            dst = y_bf[0][:, c * CH : (c + 1) * CH, :] if c < 2 else y_bf[c - 1][:]
-            nc.vector.tensor_copy(
-                out=dst.rearrange("p (g i) t -> p g t i", i=LINE),
-                in_=y[c].rearrange("p t (g i) -> p g t i", i=LINE),
+        def round_y(k, j0, j1, move):
+            move(
+                out=y_bf[k][:, j0:j1, :].rearrange("p (g i) t -> p g t i", i=LINE),
+                in_=(y_first, y_late)[k][:, :, j0:j1].rearrange("p t (g i) -> p g t i", i=LINE),
             )
 
-        def quant_y(k):
-            js = slice(spans[k][0], spans[k][1])
+        def quant_y(k, j0, j1):
+            js = slice(spans[k][0] + j0, spans[k][0] + j1)
             nc.vector.quantize_mx(
-                out=y_codes[:, js].bitcast(FP8X4), scales=y_scales[:, js], in_=y_bf[k][:].rearrange("p j t -> p (j t)")
+                out=y_codes[:, js].bitcast(FP8X4),
+                scales=y_scales[:, js],
+                in_=y_bf[k][:, j0:j1, :].rearrange("p j t -> p (j t)"),
             )
 
         sums = [psum.tile([P, 2, P], F32, name=f"sums{u}", tag=f"turn{u}") for u in range(2)]
@@ -214,26 +211,30 @@ def tile_attend_headmerge_pl_kernel(tc, keys, ka, kb, wd, offs, offs2, out_0, ou
         deal_w(1, 0, 2)
         deal_w(1, 2, PACK)
         weave()
-        merge(0)
-        merge(1)
-        quant_x(0)
-        quant_x(1)
-        quant_w(0)
-        project_first(0)
-        quant_w(1)
-        project_first(1)
-        merge(3)
-        quant_x(2)
-        project_late(1)
-        quant_x(3)
-        project_late(2)
-        round_y(0)
-        round_y(1)
-        round_y(2)
-        quant_y(0)
-        quant_y(1)
+        for c in range(2):
+            merge(x_bf[0][:, c * CH : (c + 1) * CH, :], c * CH, (c + 1) * CH)
+        for c in range(2):
+            quant_x(0, c * CH, (c + 1) * CH, x_bf[0][:, c * CH : (c + 1) * CH, :])
+        for t in range(PACK):
+            quant_w(t, t + 1)
+            project_first(t, t + 1)
+            if t % 2:
+                merge(x_last[t // 2], 3 * CH + t // 2 * CH // 2, 3 * CH + (t // 2 + 1) * CH // 2)
+        quant_x(1, 0, CH, x_bf[1][:])
+        for h in range(2):
+            quant_x(1, CH + h * CH // 2, CH + (h + 1) * CH // 2, x_last[h])
+        project_late(0, 2, nc.scalar.copy, "turn1")
+        project_late(2, 3, nc.scalar.copy, "acc_late2")
+        round_y(0, 0, CH, nc.vector.tensor_copy)
+        project_late(3, PACK, nc.vector.tensor_copy, "acc_late3")
+        round_y(0, CH, HALF, nc.vector.tensor_copy)
+        quant_y(0, 0, CH)
+        round_y(1, 0, CH, nc.vector.tensor_copy)
+        round_y(1, CH, HALF, nc.scalar.copy)
+        quant_y(0, CH, HALF)
+        quant_y(1, 0, CH)
         nc.sync.dma_start(out=word_rows[:, : 3 * CH], in_=y_codes[:, : 3 * CH])
-        quant_y(2)
+        quant_y(1, CH, HALF)
         nc.sync.dma_start(out=word_rows[:, 3 * CH :], in_=y_codes[:, 3 * CH :])
         for q in range(4):
             queue = nc.scalar if q % 2 else nc.sync

@@ -161,19 +161,19 @@ def tile_attend_headmerge_pl_kernel(tc, keys, ka, kb, wd, offs, offs2, out_0, ou
                 stop=True,
             )
 
-        def project_first(t0, t1):
-            acc = psum.tile([P, t1 - t0, HALF], F32, name=f"acc_first{t0}", tag="turn0" if t0 == 0 else f"acc_first{t0}")
+        def project(k, t0, t1, tag):
+            acc = psum.tile([P, t1 - t0, HALF], F32, name=f"acc{k}{t0}", tag=tag)
             for t in range(t0, t1):
-                product(acc[:, t - t0, :], t, 0)
-            nc.scalar.copy(out=y_first[:, t0:t1, :], in_=acc[:])
-            nc.sync.dma_start(out=y_rows[:, t0:t1, :HALF], in_=y_first[:, t0:t1, :])
+                product(acc[:, t - t0, :], t, k)
+            return acc
 
-        def project_late(t0, t1, move, tag):
-            acc = psum.tile([P, t1 - t0, HALF], F32, name=f"acc_late{t0}", tag=tag)
-            for t in range(t0, t1):
-                product(acc[:, t - t0, :], t, 1)
-            move(out=y_late[:, t0:t1, :], in_=acc[:])
-            nc.sync.dma_start(out=y_rows[:, t0:t1, HALF:], in_=y_late[:, t0:t1, :])
+        def empty(k, t0, t1, acc, move):
+            move(out=(y_first, y_late)[k][:, t0:t1, :], in_=acc[:])
+
+        def store(k, t0, t1):
+            nc.sync.dma_start(
+                out=y_rows[:, t0:t1, k * HALF : (k + 1) * HALF], in_=(y_first, y_late)[k][:, t0:t1, :]
+            )
 
         def round_y(k, j0, j1, move):
             move(
@@ -215,18 +215,23 @@ def tile_attend_headmerge_pl_kernel(tc, keys, ka, kb, wd, offs, offs2, out_0, ou
             merge(x_bf[0][:, c * CH : (c + 1) * CH, :], c * CH, (c + 1) * CH)
         for c in range(2):
             quant_x(0, c * CH, (c + 1) * CH, x_bf[0][:, c * CH : (c + 1) * CH, :])
+        first = []
         for t in range(PACK):
             quant_w(t, t + 1)
-            project_first(t, t + 1)
+            first.append(project(0, t, t + 1, "turn0" if t == 0 else f"first{t}"))
+            empty(0, t, t + 1, first[t], nc.scalar.copy)
+            store(0, t, t + 1)
             if t % 2:
                 merge(x_last[t // 2], 3 * CH + t // 2 * CH // 2, 3 * CH + (t // 2 + 1) * CH // 2)
         quant_x(1, 0, CH, x_bf[1][:])
         for h in range(2):
             quant_x(1, CH + h * CH // 2, CH + (h + 1) * CH // 2, x_last[h])
-        project_late(0, 2, nc.scalar.copy, "turn1")
-        project_late(2, 3, nc.scalar.copy, "acc_late2")
+        empty(1, 0, 2, project(1, 0, 2, "turn1"), nc.scalar.copy)
+        store(1, 0, 2)
+        empty(1, 2, 3, project(1, 2, 3, "late2"), nc.scalar.copy)
         round_y(0, 0, CH, nc.vector.tensor_copy)
-        project_late(3, PACK, nc.vector.tensor_copy, "acc_late3")
+        empty(1, 3, PACK, project(1, 3, PACK, "late3"), nc.vector.tensor_copy)
+        store(1, 2, PACK)
         round_y(0, CH, HALF, nc.vector.tensor_copy)
         quant_y(0, 0, CH)
         round_y(1, 0, CH, nc.vector.tensor_copy)

@@ -88,7 +88,7 @@ def tile_attend_headmerge_pl_kernel(tc, keys, ka, kb, wd, offs, offs2, out_0, ou
         w_bf = keep.tile([P, PACK, P, PACK], BF16, name="w_bf", align_bytes=64)
         x_last = [w_bf[:, 2 * h, : CH // 2, :] for h in range(2)]
         turned = slice(HALF, HALF + CH)
-        back = psum.tile([P, 2, CH], F32, name="back")
+        back = psum.tile([P, 2, CH], F32, name="back", tag="back")
 
         def sum_turned(dst, t):
             for s, term in enumerate((term_a, term_b)):
@@ -226,12 +226,12 @@ def tile_attend_headmerge_pl_kernel(tc, keys, ka, kb, wd, offs, offs2, out_0, ou
         quant_x(1, 0, CH, x_bf[1][:])
         for h in range(2):
             quant_x(1, CH + h * CH // 2, CH + (h + 1) * CH // 2, x_last[h])
-        empty(1, 0, 2, project(1, 0, 2, "turn1"), nc.scalar.copy)
-        store(1, 0, 2)
-        empty(1, 2, 3, project(1, 2, 3, "late2"), nc.scalar.copy)
+        for t, tag in enumerate(("turn1", "back", "late2")):
+            empty(1, t, t + 1, project(1, t, t + 1, tag), nc.scalar.copy)
+            store(1, t, t + 1)
         round_y(0, 0, CH, nc.vector.tensor_copy)
         empty(1, 3, PACK, project(1, 3, PACK, "late3"), nc.vector.tensor_copy)
-        store(1, 2, PACK)
+        store(1, 3, PACK)
         round_y(0, CH, HALF, nc.vector.tensor_copy)
         quant_y(0, 0, CH)
         round_y(1, 0, CH, nc.vector.tensor_copy)

@@ -220,7 +220,8 @@ def tile_attend_headmerge_pl_kernel(tc, keys, ka, kb, wd, offs, offs2, out_0, ou
             quant_w(t, t + 1)
             first.append(project(0, t, t + 1, "turn0" if t == 0 else f"first{t}"))
             empty(0, t, t + 1, first[t], nc.scalar.copy)
-            store(0, t, t + 1)
+            if t:
+                store(0, 0 if t == 1 else t, t + 1)
             if t % 2:
                 merge(x_last[t // 2], 3 * CH + t // 2 * CH // 2, 3 * CH + (t // 2 + 1) * CH // 2)
         quant_x(1, 0, CH, x_bf[1][:])

@@ -24,6 +24,7 @@ LINE = 4
 HALF = J // 2
 ON_SCALAR = 0
 LEAD = T // 4
+SPLIT = 176
 
 
 def tile_attend_headmerge_pl_kernel(tc, keys, ka, kb, wd, offs, offs2, out_0, out_1, out_2):
@@ -227,21 +228,20 @@ def tile_attend_headmerge_pl_kernel(tc, keys, ka, kb, wd, offs, offs2, out_0, ou
         quant_x(1, 0, CH, x_bf[1][:])
         for h in range(2):
             quant_x(1, CH + h * CH // 2, CH + (h + 1) * CH // 2, x_last[h])
-        for t, tag in enumerate(("turn1", "back", "late2")):
+        for t, tag in enumerate(("turn1", "back", "late2", "late3")):
             empty(1, t, t + 1, project(1, t, t + 1, tag), nc.scalar.copy)
             store(1, t, t + 1)
         round_y(0, 0, CH, nc.vector.tensor_copy)
-        empty(1, 3, PACK, project(1, 3, PACK, "late3"), nc.vector.tensor_copy)
-        store(1, 3, PACK)
         round_y(0, CH, HALF, nc.vector.tensor_copy)
         quant_y(0, 0, CH)
-        round_y(1, 0, CH, nc.vector.tensor_copy)
-        round_y(1, CH, HALF, nc.scalar.copy)
         quant_y(0, CH, HALF)
+        nc.sync.dma_start(out=word_rows[:, :HALF], in_=y_codes[:, :HALF])
+        round_y(1, 0, CH, nc.vector.tensor_copy)
+        round_y(1, CH, SPLIT, nc.vector.tensor_copy)
+        round_y(1, SPLIT, HALF, nc.scalar.copy)
         quant_y(1, 0, CH)
-        nc.sync.dma_start(out=word_rows[:, : 3 * CH], in_=y_codes[:, : 3 * CH])
         quant_y(1, CH, HALF)
-        nc.sync.dma_start(out=word_rows[:, 3 * CH :], in_=y_codes[:, 3 * CH :])
+        nc.sync.dma_start(out=word_rows[:, HALF:], in_=y_codes[:, HALF:])
         for q in range(4):
             queue = nc.scalar if q % 2 else nc.sync
             queue.dma_start(out=scale_rows[4 * q : 4 * q + 4, :], in_=y_scales[32 * q : 32 * q + 4, :].bitcast(I32))

@@ -59,7 +59,8 @@ def tile_attend_headmerge_pl_kernel(tc, keys, ka, kb, wd, offs, offs2, out_0, ou
         for t in range(1, PACK):
             nc.sync.dma_start(out=planes[t][:], in_=key_rows[:, t, :])
         for h in range(2):
-            nc.sync.dma_start(out=w_raw[h][:], in_=w_rows[:, :, h * C // 2 : (h + 1) * C // 2])
+            for r in range(0, PACK, 2):
+                nc.sync.dma_start(out=w_raw[h][:, r : r + 2, :], in_=w_rows[:, r : r + 2, h * C // 2 : (h + 1) * C // 2])
 
         ident = keep.tile([P, P], F32, name="ident")
         make_identity(nc, ident[:])

@@ -22,9 +22,9 @@ CH = 128
 NCH = J // CH
 LINE = 4
 HALF = J // 2
-ON_SCALAR = 0
 LEAD = T // 4
 SPLIT = 176
+DEAL_S = 48
 
 
 def tile_attend_headmerge_pl_kernel(tc, keys, ka, kb, wd, offs, offs2, out_0, out_1, out_2):
@@ -40,7 +40,7 @@ def tile_attend_headmerge_pl_kernel(tc, keys, ka, kb, wd, offs, offs2, out_0, ou
         key_rows = keys.rearrange("(p t) n -> p t n", t=PACK)
         w_rows = wd.rearrange("(p r) c -> p r c", r=PACK)
         w_raw = [
-            stage.tile([P, PACK, C // 2], F32, name="w_raw0", align_bytes=64, offset=J * 4 + C * 8),
+            keep.tile([P, PACK, C // 2], F32, name="w_raw0"),
             keep.tile([P, PACK, C // 2], F32, name="w_raw1"),
         ]
         term_a = keep.tile([P, PACK, J], F32, name="term_a")
@@ -68,21 +68,23 @@ def tile_attend_headmerge_pl_kernel(tc, keys, ka, kb, wd, offs, offs2, out_0, ou
         for s in range(2):
             for i in range(PACK):
                 nc.tensor.transpose(spread[s][:, i, :], cols[s][:, i : i + 1].to_broadcast([P, P]), ident[:])
-        shares = [keep.tile([P, J], F32, name=f"share{s}") for s in range(2)]
-        for s, move in enumerate((nc.scalar.copy, nc.vector.tensor_copy)):
-            move(out=shares[s][:].rearrange("m (p i) -> m p i", i=PACK), in_=spread[s][:].rearrange("m i p -> m p i"))
+        share_a = keep.tile([P, J], F32, name="share_a")
+        nc.scalar.copy(out=share_a[:].rearrange("m (p i) -> m p i", i=PACK), in_=spread[0][:].rearrange("m i p -> m p i"))
+        share_b = spread[1][:].rearrange("m i p -> m p i")
 
         def gather_a(t):
-            nc.vector.tensor_tensor(term_a[:, t, :], planes[t][:].indirect(list_a[:]), shares[0][:], MULT)
+            nc.vector.tensor_tensor(term_a[:, t, :], planes[t][:].indirect(list_a[:]), share_a[:], MULT)
 
         def gather_b(t):
-            if t < ON_SCALAR:
-                nc.vector.tensor_tensor(term_b[:, t, :], planes[t][:].indirect(list_b[:]), shares[1][:], MULT)
-            else:
-                nc.scalar.activation(raw[t], planes[t][:].indirect(list_b[:]), COPY)
+            nc.scalar.activation(raw[t], planes[t][:].indirect(list_b[:]), COPY)
 
         def scale_b(t, j0, j1):
-            nc.vector.tensor_tensor(term_b[:, t, j0:j1], raw[t][:, j0:j1], shares[1][:, j0:j1], MULT)
+            nc.vector.tensor_tensor(
+                term_b[:, t, j0:j1].rearrange("m (p i) -> m p i", i=PACK),
+                raw[t][:, j0:j1].rearrange("m (p i) -> m p i", i=PACK),
+                share_b[:, j0 // PACK : j1 // PACK, :],
+                MULT,
+            )
 
         spans = ((0, HALF), (HALF, J))
         x_bf = [keep.tile([P, HALF, PACK], BF16, name="x_bf_first", align_bytes=64)]
@@ -99,8 +101,8 @@ def tile_attend_headmerge_pl_kernel(tc, keys, ka, kb, wd, offs, offs2, out_0, ou
                 )
 
         def pair_back(u, bank, pairs):
-            nc.scalar.copy(out=pairs[:], in_=bank[:].rearrange("j e p -> j p e"))
-            nc.tensor.transpose(back[:, u, :], pairs[:].rearrange("j p e -> j (p e)").bitcast(F32), ident[:])
+            nc.scalar.copy(out=pairs, in_=bank[:].rearrange("j e p -> j p e"))
+            nc.tensor.transpose(back[:, u, :], pairs.rearrange("j p e -> j (p e)").bitcast(F32), ident[:])
 
         def weave():
             words = x_bf[1][:].rearrange("p j t -> p (j t)").bitcast(F32).rearrange("p (j u) -> p j u", u=2)
@@ -108,11 +110,11 @@ def tile_attend_headmerge_pl_kernel(tc, keys, ka, kb, wd, offs, offs2, out_0, ou
         x_codes = [keep.tile([P, j1 - j0], I32, name=f"x_codes{j0}", align_bytes=64) for j0, j1 in spans]
         x_scales = [keep.tile([P, j1 - j0], U8, name=f"x_scales{j0}", align_bytes=64) for j0, j1 in spans]
 
-        def merge(dst, j0, j1):
+        def merge(dst, j0, j1, t0=0, t1=PACK):
             nc.vector.tensor_tensor(
-                dst.rearrange("p (g i) t -> p g t i", i=LINE),
-                term_a[:, :, j0:j1].rearrange("p t (g i) -> p g t i", i=LINE),
-                term_b[:, :, j0:j1].rearrange("p t (g i) -> p g t i", i=LINE),
+                dst[:, :, t0:t1].rearrange("p (g i) t -> p g t i", i=LINE),
+                term_a[:, t0:t1, j0:j1].rearrange("p t (g i) -> p g t i", i=LINE),
+                term_b[:, t0:t1, j0:j1].rearrange("p t (g i) -> p g t i", i=LINE),
                 ADD,
             )
 
@@ -128,10 +130,10 @@ def tile_attend_headmerge_pl_kernel(tc, keys, ka, kb, wd, offs, offs2, out_0, ou
         ]
         w_scales = [keep.tile([P, 2 * P], U8, name=f"w_scales{u}", align_bytes=64) for u in range(2)]
 
-        def deal_w(h, t0, t1):
-            nc.scalar.copy(
-                out=w_bf[:, t0:t1, h * P // 2 : (h + 1) * P // 2, :].rearrange("p t m r -> p m r t"),
-                in_=w_raw[h][:].rearrange("p r (m t) -> p m r t", t=PACK)[:, :, :, t0:t1],
+        def deal_w(h, t0, t1, m0=0, m1=P // 2, move=nc.scalar.copy):
+            move(
+                out=w_bf[:, t0:t1, h * P // 2 + m0 : h * P // 2 + m1, :].rearrange("p t m r -> p m r t"),
+                in_=w_raw[h][:].rearrange("p r (m t) -> p m r t", t=PACK)[:, m0:m1, :, t0:t1],
             )
 
         def quant_w(t0, t1):
@@ -191,30 +193,33 @@ def tile_attend_headmerge_pl_kernel(tc, keys, ka, kb, wd, offs, offs2, out_0, ou
                 in_=y_bf[k][:, j0:j1, :].rearrange("p j t -> p (j t)"),
             )
 
-        sums = [psum.tile([P, 2, P], F32, name=f"sums{u}", tag=f"turn{u}") for u in range(2)]
+        sums = [psum.tile([P, 2, P], F32, name=f"sums{u}", tag=("turn0", "late3")[u]) for u in range(2)]
         pairs = [
-            keep.tile([P, P, 2], BF16, name="pairs0"),
-            stage.tile([P, P, 2], BF16, name="pairs1", align_bytes=64, offset=J * 4 + C * 8),
+            keep.tile([P, P, 2], BF16, name="pairs0")[:],
+            w_raw[0][:, 0, :P].bitcast(BF16).rearrange("j (p e) -> j p e", e=2),
         ]
         for t in range(PACK):
             gather_a(t)
             gather_b(t)
             if t == 2:
                 pair_back(0, sums[0], pairs[0])
-            if ON_SCALAR <= t < PACK - 1:
+            if t < PACK - 1:
                 scale_b(t, 0, J)
             if t < PACK - 1:
                 sum_turned(sums[t // 2][:, t % 2, :], t)
+            if t == 1:
+                merge(x_bf[0][:, :CH, :], 0, CH, 0, 2)
         scale_b(PACK - 1, 0, HALF)
         scale_b(PACK - 1, HALF, J)
         sum_turned(sums[1][:, 1, :], PACK - 1)
         deal_w(0, 0, PACK)
         pair_back(1, sums[1], pairs[1])
-        deal_w(1, 0, 2)
-        deal_w(1, 2, PACK)
+        deal_w(1, 0, 2, 0, DEAL_S)
+        deal_w(1, 2, PACK, 0, DEAL_S)
         weave()
         for c in range(2):
-            merge(x_bf[0][:, c * CH : (c + 1) * CH, :], c * CH, (c + 1) * CH)
+            merge(x_bf[0][:, c * CH : (c + 1) * CH, :], c * CH, (c + 1) * CH, 2 - 2 * c, PACK)
+        deal_w(1, 0, PACK, DEAL_S, P // 2, nc.vector.tensor_copy)
         for c in range(2):
             quant_x(0, c * CH, (c + 1) * CH, x_bf[0][:, c * CH : (c + 1) * CH, :])
         first = []

@@ -172,7 +172,9 @@ def tile_attend_headmerge_pl_kernel(tc, keys, ka, kb, wd, offs, offs2, out_0, ou
             return acc
 
         def empty(k, t0, t1, acc, move):
-            move(out=(y_first, y_late)[k][:, t0:t1, :], in_=acc[:])
+            cuts = (0, CH, HALF) if t1 == PACK else (0, HALF)
+            for j0, j1 in zip(cuts, cuts[1:]):
+                move(out=(y_first, y_late)[k][:, t0:t1, j0:j1], in_=acc[:, :, j0:j1])
 
         def store(k, t0, t1):
             nc.sync.dma_start(

@@ -19,12 +19,13 @@ COPY = mybir.ActivationFunctionType.Copy
 P = 128
 PACK = 4
 CH = 128
-NCH = J // CH
 LINE = 4
 HALF = J // 2
+W_HALF = P // 2
 LEAD = T // 4
 SPLIT = 176
 DEAL_S = 48
+EARLY = 192
 
 
 def tile_attend_headmerge_pl_kernel(tc, keys, ka, kb, wd, offs, offs2, out_0, out_1, out_2):
@@ -36,13 +37,10 @@ def tile_attend_headmerge_pl_kernel(tc, keys, ka, kb, wd, offs, offs2, out_0, ou
 
         list_a = keep.tile([P, J // 16], U16, name="list_a")
         list_b = keep.tile([P, J // 16], U16, name="list_b")
-        planes = [keep.tile([P, T], F32, name=f"plane{t}") for t in range(PACK)]
+        windows = [keep.tile([P, T], F32, name=f"window{t}") for t in range(PACK)]
         key_rows = keys.rearrange("(p t) n -> p t n", t=PACK)
         w_rows = wd.rearrange("(p r) c -> p r c", r=PACK)
-        w_raw = [
-            keep.tile([P, PACK, C // 2], F32, name="w_raw0"),
-            keep.tile([P, PACK, C // 2], F32, name="w_raw1"),
-        ]
+        w_raw = [keep.tile([P, PACK, C // 2], F32, name=f"w_raw{h}") for h in range(2)]
         term_a = keep.tile([P, PACK, J], F32, name="term_a")
         term_b = keep.tile([P, PACK, J], F32, name="term_b")
         raw_early = keep.tile([P, 3 * J], F32, name="raw_early")
@@ -50,14 +48,14 @@ def tile_attend_headmerge_pl_kernel(tc, keys, ka, kb, wd, offs, offs2, out_0, ou
         raw = [raw_early[:, :J], raw_early[:, J : 2 * J], raw_early[:, 2 * J :], raw_last[:]]
         cols = [keep.tile([P, PACK], F32, name="cols_a")[:], raw_early[:, J - 2 : J + 2]]
 
-        nc.sync.dma_start(out=planes[0][:, :LEAD], in_=key_rows[:, 0, :LEAD])
+        nc.sync.dma_start(out=windows[0][:, :LEAD], in_=key_rows[:, 0, :LEAD])
         for s, share in enumerate((ka, kb)):
             nc.sync.dma_start(out=cols[s], in_=share.rearrange("o (p i) -> p (o i)", i=PACK))
         nc.sync.dma_start(list_a[:], offs)
         nc.sync.dma_start(list_b[:], offs2)
-        nc.sync.dma_start(out=planes[0][:, LEAD:], in_=key_rows[:, 0, LEAD:])
+        nc.sync.dma_start(out=windows[0][:, LEAD:], in_=key_rows[:, 0, LEAD:])
         for t in range(1, PACK):
-            nc.sync.dma_start(out=planes[t][:], in_=key_rows[:, t, :])
+            nc.sync.dma_start(out=windows[t][:], in_=key_rows[:, t, :])
         for h in range(2):
             for r in range(0, PACK, 2):
                 nc.sync.dma_start(out=w_raw[h][:, r : r + 2, :], in_=w_rows[:, r : r + 2, h * C // 2 : (h + 1) * C // 2])
@@ -73,10 +71,10 @@ def tile_attend_headmerge_pl_kernel(tc, keys, ka, kb, wd, offs, offs2, out_0, ou
         share_b = spread[1][:].rearrange("m i p -> m p i")
 
         def gather_a(t):
-            nc.vector.tensor_tensor(term_a[:, t, :], planes[t][:].indirect(list_a[:]), share_a[:], MULT)
+            nc.vector.tensor_tensor(term_a[:, t, :], windows[t][:].indirect(list_a[:]), share_a[:], MULT)
 
         def gather_b(t):
-            nc.scalar.activation(raw[t], planes[t][:].indirect(list_b[:]), COPY)
+            nc.scalar.activation(raw[t], windows[t][:].indirect(list_b[:]), COPY)
 
         def scale_b(t, j0, j1):
             nc.vector.tensor_tensor(
@@ -86,9 +84,8 @@ def tile_attend_headmerge_pl_kernel(tc, keys, ka, kb, wd, offs, offs2, out_0, ou
                 MULT,
             )
 
-        spans = ((0, HALF), (HALF, J))
-        x_bf = [keep.tile([P, HALF, PACK], BF16, name="x_bf_first", align_bytes=64)]
-        x_bf.append(keep.tile([P, CH, PACK], BF16, name="x_bf_turned", align_bytes=64))
+        x_first = keep.tile([P, HALF, PACK], BF16, name="x_first", align_bytes=64)
+        x_turned = keep.tile([P, CH, PACK], BF16, name="x_turned", align_bytes=64)
         w_bf = keep.tile([P, PACK, P, PACK], BF16, name="w_bf", align_bytes=64)
         x_last = [w_bf[:, 2 * h, : CH // 2, :] for h in range(2)]
         turned = slice(HALF, HALF + CH)
@@ -100,15 +97,16 @@ def tile_attend_headmerge_pl_kernel(tc, keys, ka, kb, wd, offs, offs2, out_0, ou
                     dst, lhsT=term[:, t, turned], rhs=ident[:], is_transpose=True, start=(s == 0), stop=(s == 1)
                 )
 
-        def pair_back(u, bank, pairs):
-            nc.scalar.copy(out=pairs, in_=bank[:].rearrange("j e p -> j p e"))
-            nc.tensor.transpose(back[:, u, :], pairs.rearrange("j p e -> j (p e)").bitcast(F32), ident[:])
+        def pair_back(u, bank, pair_tile):
+            nc.scalar.copy(out=pair_tile, in_=bank[:].rearrange("j e p -> j p e"))
+            nc.tensor.transpose(back[:, u, :], pair_tile.rearrange("j p e -> j (p e)").bitcast(F32), ident[:])
 
         def weave():
-            words = x_bf[1][:].rearrange("p j t -> p (j t)").bitcast(F32).rearrange("p (j u) -> p j u", u=2)
-            nc.scalar.copy(out=words, in_=back[:].rearrange("p u j -> p j u"))
-        x_codes = [keep.tile([P, j1 - j0], I32, name=f"x_codes{j0}", align_bytes=64) for j0, j1 in spans]
-        x_scales = [keep.tile([P, j1 - j0], U8, name=f"x_scales{j0}", align_bytes=64) for j0, j1 in spans]
+            pair_words = x_turned[:].rearrange("p j t -> p (j t)").bitcast(F32).rearrange("p (j u) -> p j u", u=2)
+            nc.scalar.copy(out=pair_words, in_=back[:].rearrange("p u j -> p j u"))
+
+        x_codes = [keep.tile([P, HALF], I32, name=f"x_codes{k}", align_bytes=64) for k in range(2)]
+        x_scales = [keep.tile([P, HALF], U8, name=f"x_scales{k}", align_bytes=64) for k in range(2)]
 
         def merge(dst, j0, j1, t0=0, t1=PACK):
             nc.vector.tensor_tensor(
@@ -130,33 +128,33 @@ def tile_attend_headmerge_pl_kernel(tc, keys, ka, kb, wd, offs, offs2, out_0, ou
         ]
         w_scales = [keep.tile([P, 2 * P], U8, name=f"w_scales{u}", align_bytes=64) for u in range(2)]
 
-        def deal_w(h, t0, t1, m0=0, m1=P // 2, move=nc.scalar.copy):
+        def deal_w(h, t0, t1, m0, m1, move):
             move(
-                out=w_bf[:, t0:t1, h * P // 2 + m0 : h * P // 2 + m1, :].rearrange("p t m r -> p m r t"),
+                out=w_bf[:, t0:t1, h * W_HALF + m0 : h * W_HALF + m1, :].rearrange("p t m r -> p m r t"),
                 in_=w_raw[h][:].rearrange("p r (m t) -> p m r t", t=PACK)[:, m0:m1, :, t0:t1],
             )
 
-        def quant_w(t0, t1):
-            ms = slice(t0 % 2 * P, ((t1 - 1) % 2 + 1) * P)
+        def quant_w(t):
+            ms = slice(t % 2 * P, (t % 2 + 1) * P)
             nc.vector.quantize_mx(
-                out=w_codes[t0 // 2][:, ms].bitcast(FP8X4),
-                scales=w_scales[t0 // 2][:, ms],
-                in_=w_bf[:, t0:t1, :, :].rearrange("p t m r -> p (t m r)"),
+                out=w_codes[t // 2][:, ms].bitcast(FP8X4),
+                scales=w_scales[t // 2][:, ms],
+                in_=w_bf[:, t, :, :].rearrange("p m r -> p (m r)"),
             )
 
-        y_first = keep.tile([P, PACK, HALF], F32, name="y_first")
-        y_late = keep.tile([P, PACK, HALF], F32, name="y_late")
-        y_bf = [keep.tile([P, j1 - j0, PACK], BF16, name=f"y_bf{j0}", align_bytes=64) for j0, j1 in spans]
+        y_half = [keep.tile([P, PACK, HALF], F32, name=f"y_half{k}") for k in range(2)]
+        y_bf = [keep.tile([P, HALF, PACK], BF16, name=f"y_bf{k}", align_bytes=64) for k in range(2)]
         y_codes = keep.tile([P, J], I32, name="y_codes", align_bytes=64)
         y_scales = keep.tile([P, J], U8, name="y_scales", align_bytes=64)
         y_rows = out_0.rearrange("(p t) j -> p t j", t=PACK)
         word_rows = out_1[0].rearrange("l c r -> l (c r)").bitcast(I32)
         scale_rows = out_2[0].bitcast(I32)
 
-        def product(dst, t, k):
+        def project(k, t, tag):
             ms = slice(t % 2 * P, (t % 2 + 1) * P)
+            acc = psum.tile([P, HALF], F32, name=f"acc{k}{t}", tag=tag)
             nc.tensor.matmul_mx(
-                out=dst,
+                out=acc[:],
                 lhsT=w_codes[t // 2][:, ms].bitcast(FP8X4),
                 lhsT_scale=w_scales[t // 2][:, ms],
                 rhs=x_codes[k][:].bitcast(FP8X4),
@@ -164,92 +162,84 @@ def tile_attend_headmerge_pl_kernel(tc, keys, ka, kb, wd, offs, offs2, out_0, ou
                 start=True,
                 stop=True,
             )
-
-        def project(k, t0, t1, tag):
-            acc = psum.tile([P, t1 - t0, HALF], F32, name=f"acc{k}{t0}", tag=tag)
-            for t in range(t0, t1):
-                product(acc[:, t - t0, :], t, k)
-            return acc
-
-        def empty(k, t0, t1, acc, move):
-            cuts = (0, CH, HALF) if t1 == PACK else (0, HALF)
+            cuts = (0, CH, HALF) if t == PACK - 1 else (0, HALF)
             for j0, j1 in zip(cuts, cuts[1:]):
-                move(out=(y_first, y_late)[k][:, t0:t1, j0:j1], in_=acc[:, :, j0:j1])
+                nc.scalar.copy(out=y_half[k][:, t, j0:j1], in_=acc[:, j0:j1])
 
         def store(k, t0, t1):
-            nc.sync.dma_start(
-                out=y_rows[:, t0:t1, k * HALF : (k + 1) * HALF], in_=(y_first, y_late)[k][:, t0:t1, :]
-            )
+            nc.sync.dma_start(out=y_rows[:, t0:t1, k * HALF : (k + 1) * HALF], in_=y_half[k][:, t0:t1, :])
 
         def round_y(k, j0, j1, move):
             move(
                 out=y_bf[k][:, j0:j1, :].rearrange("p (g i) t -> p g t i", i=LINE),
-                in_=(y_first, y_late)[k][:, :, j0:j1].rearrange("p t (g i) -> p g t i", i=LINE),
+                in_=y_half[k][:, :, j0:j1].rearrange("p t (g i) -> p g t i", i=LINE),
             )
 
-        def quant_y(k, j0, j1):
-            js = slice(spans[k][0] + j0, spans[k][0] + j1)
-            nc.vector.quantize_mx(
-                out=y_codes[:, js].bitcast(FP8X4),
-                scales=y_scales[:, js],
-                in_=y_bf[k][:, j0:j1, :].rearrange("p j t -> p (j t)"),
-            )
+        def planes_out(k):
+            for j0 in range(0, HALF, CH):
+                js = slice(k * HALF + j0, k * HALF + j0 + CH)
+                nc.vector.quantize_mx(
+                    out=y_codes[:, js].bitcast(FP8X4),
+                    scales=y_scales[:, js],
+                    in_=y_bf[k][:, j0 : j0 + CH, :].rearrange("p j t -> p (j t)"),
+                )
+            nc.sync.dma_start(out=word_rows[:, k * HALF : (k + 1) * HALF], in_=y_codes[:, k * HALF : (k + 1) * HALF])
 
         sums = [psum.tile([P, 2, P], F32, name=f"sums{u}", tag=("turn0", "late3")[u]) for u in range(2)]
         pairs = [
             keep.tile([P, P, 2], BF16, name="pairs0")[:],
             w_raw[0][:, 0, :P].bitcast(BF16).rearrange("j (p e) -> j p e", e=2),
         ]
+        last = PACK - 1
         for t in range(PACK):
             gather_a(t)
             gather_b(t)
             if t == 2:
                 pair_back(0, sums[0], pairs[0])
-            if t < PACK - 1:
+            if t < last:
                 scale_b(t, 0, J)
-            if t < PACK - 1:
                 sum_turned(sums[t // 2][:, t % 2, :], t)
             if t == 1:
-                merge(x_bf[0][:, :CH, :], 0, CH, 0, 2)
-        scale_b(PACK - 1, 0, HALF)
-        scale_b(PACK - 1, HALF, J)
-        sum_turned(sums[1][:, 1, :], PACK - 1)
-        deal_w(0, 0, PACK)
+                merge(x_first[:, :EARLY, :], 0, EARLY, 0, 2)
+
+        scale_b(last, 0, HALF)
+        scale_b(last, HALF, J)
+        sum_turned(sums[1][:, 1, :], last)
+        deal_w(0, 0, PACK, 0, W_HALF, nc.scalar.copy)
         pair_back(1, sums[1], pairs[1])
-        deal_w(1, 0, 2, 0, DEAL_S)
-        deal_w(1, 2, PACK, 0, DEAL_S)
+        deal_w(1, 0, 2, 0, DEAL_S, nc.scalar.copy)
+        deal_w(1, 2, PACK, 0, DEAL_S, nc.scalar.copy)
         weave()
-        for c in range(2):
-            merge(x_bf[0][:, c * CH : (c + 1) * CH, :], c * CH, (c + 1) * CH, 2 - 2 * c, PACK)
-        deal_w(1, 0, PACK, DEAL_S, P // 2, nc.vector.tensor_copy)
-        for c in range(2):
-            quant_x(0, c * CH, (c + 1) * CH, x_bf[0][:, c * CH : (c + 1) * CH, :])
-        first = []
-        for t in range(PACK):
-            quant_w(t, t + 1)
-            first.append(project(0, t, t + 1, "turn0" if t == 0 else f"first{t}"))
-            empty(0, t, t + 1, first[t], nc.scalar.copy)
+        merge(x_first[:, :EARLY, :], 0, EARLY, 2, PACK)
+        merge(x_first[:, EARLY:, :], EARLY, HALF)
+        deal_w(1, 0, PACK, DEAL_S, W_HALF, nc.vector.tensor_copy)
+        for j0 in range(0, HALF, CH):
+            quant_x(0, j0, j0 + CH, x_first[:, j0 : j0 + CH, :])
+
+        for t, tag in enumerate(("turn0", "first1", "first2", "first3")):
+            quant_w(t)
+            project(0, t, tag)
             if t:
                 store(0, 0 if t == 1 else t, t + 1)
             if t % 2:
-                merge(x_last[t // 2], 3 * CH + t // 2 * CH // 2, 3 * CH + (t // 2 + 1) * CH // 2)
-        quant_x(1, 0, CH, x_bf[1][:])
+                j0 = HALF + CH + t // 2 * CH // 2
+                merge(x_last[t // 2], j0, j0 + CH // 2)
+        quant_x(1, 0, CH, x_turned[:])
         for h in range(2):
             quant_x(1, CH + h * CH // 2, CH + (h + 1) * CH // 2, x_last[h])
+
         for t, tag in enumerate(("turn1", "back", "late2", "late3")):
-            empty(1, t, t + 1, project(1, t, t + 1, tag), nc.scalar.copy)
+            project(1, t, tag)
             store(1, t, t + 1)
+
         round_y(0, 0, CH, nc.vector.tensor_copy)
         round_y(0, CH, HALF, nc.vector.tensor_copy)
-        quant_y(0, 0, CH)
-        quant_y(0, CH, HALF)
-        nc.sync.dma_start(out=word_rows[:, :HALF], in_=y_codes[:, :HALF])
+        planes_out(0)
         round_y(1, 0, CH, nc.vector.tensor_copy)
         round_y(1, CH, SPLIT, nc.vector.tensor_copy)
         round_y(1, SPLIT, HALF, nc.scalar.copy)
-        quant_y(1, 0, CH)
-        quant_y(1, CH, HALF)
-        nc.sync.dma_start(out=word_rows[:, HALF:], in_=y_codes[:, HALF:])
+        planes_out(1)
+
         for q in range(4):
             queue = nc.scalar if q % 2 else nc.sync
             queue.dma_start(out=scale_rows[4 * q : 4 * q + 4, :], in_=y_scales[32 * q : 32 * q + 4, :].bitcast(I32))

@@ -25,6 +25,7 @@ W_HALF = P // 2
 LEAD = T // 4
 SPLIT = 176
 DEAL_S = 48
+POOL = 384
 EARLY = 192
 
 
@@ -40,7 +41,11 @@ def tile_attend_headmerge_pl_kernel(tc, keys, ka, kb, wd, offs, offs2, out_0, ou
         windows = [keep.tile([P, T], F32, name=f"window{t}") for t in range(PACK)]
         key_rows = keys.rearrange("(p t) n -> p t n", t=PACK)
         w_rows = wd.rearrange("(p r) c -> p r c", r=PACK)
-        w_raw = [keep.tile([P, PACK, C // 2], F32, name=f"w_raw{h}") for h in range(2)]
+        w_second = keep.tile([P, PACK * C // 2 + P // 2], F32, name="w_second")
+        w_raw = [
+            keep.tile([P, PACK, C // 2], F32, name="w_first")[:],
+            w_second[:, : PACK * C // 2].rearrange("p (r c) -> p r c", r=PACK),
+        ]
         term_a = keep.tile([P, PACK, J], F32, name="term_a")
         term_b = keep.tile([P, PACK, J], F32, name="term_b")
         raw_early = keep.tile([P, 3 * J], F32, name="raw_early")
@@ -69,6 +74,8 @@ def tile_attend_headmerge_pl_kernel(tc, keys, ka, kb, wd, offs, offs2, out_0, ou
         share_a = keep.tile([P, J], F32, name="share_a")
         nc.scalar.copy(out=share_a[:].rearrange("m (p i) -> m p i", i=PACK), in_=spread[0][:].rearrange("m i p -> m p i"))
         share_b = spread[1][:].rearrange("m i p -> m p i")
+        share_b_tail = keep.tile([P, J - POOL], F32, name="share_b_tail")
+        nc.scalar.copy(out=share_b_tail[:].rearrange("m (p i) -> m p i", i=PACK), in_=share_b[:, POOL // PACK :, :])
 
         def gather_a(t):
             nc.vector.tensor_tensor(term_a[:, t, :], windows[t][:].indirect(list_a[:]), share_a[:], MULT)
@@ -83,6 +90,9 @@ def tile_attend_headmerge_pl_kernel(tc, keys, ka, kb, wd, offs, offs2, out_0, ou
                 share_b[:, j0 // PACK : j1 // PACK, :],
                 MULT,
             )
+
+        def scale_tail(t):
+            nc.gpsimd.tensor_tensor(term_b[:, t, POOL:], raw[t][:, POOL:], share_b_tail[:], MULT)
 
         x_first = keep.tile([P, HALF, PACK], BF16, name="x_first", align_bytes=64)
         x_turned = keep.tile([P, CH, PACK], BF16, name="x_turned", align_bytes=64)
@@ -123,15 +133,13 @@ def tile_attend_headmerge_pl_kernel(tc, keys, ka, kb, wd, offs, offs2, out_0, ou
                 in_=src.rearrange("p j t -> p (j t)"),
             )
 
-        w_codes = [
-            stage.tile([P, 2 * P], I32, name=f"w_codes{u}", align_bytes=64, offset=u * 2 * P * 4) for u in range(2)
-        ]
+        w_codes = [keep.tile([P, 2 * P], I32, name=f"w_codes{u}", align_bytes=64) for u in range(2)]
         w_scales = [keep.tile([P, 2 * P], U8, name=f"w_scales{u}", align_bytes=64) for u in range(2)]
 
         def deal_w(h, t0, t1, m0, m1, move):
             move(
                 out=w_bf[:, t0:t1, h * W_HALF + m0 : h * W_HALF + m1, :].rearrange("p t m r -> p m r t"),
-                in_=w_raw[h][:].rearrange("p r (m t) -> p m r t", t=PACK)[:, m0:m1, :, t0:t1],
+                in_=w_raw[h].rearrange("p r (m t) -> p m r t", t=PACK)[:, m0:m1, :, t0:t1],
             )
 
         def quant_w(t):
@@ -188,7 +196,7 @@ def tile_attend_headmerge_pl_kernel(tc, keys, ka, kb, wd, offs, offs2, out_0, ou
         sums = [psum.tile([P, 2, P], F32, name=f"sums{u}", tag=("turn0", "late3")[u]) for u in range(2)]
         pairs = [
             keep.tile([P, P, 2], BF16, name="pairs0")[:],
-            w_raw[0][:, 0, :P].bitcast(BF16).rearrange("j (p e) -> j p e", e=2),
+            w_second[:, PACK * C // 2 - P // 2 :].bitcast(BF16).rearrange("j (p e) -> j p e", e=2),
         ]
         last = PACK - 1
         for t in range(PACK):
@@ -197,22 +205,25 @@ def tile_attend_headmerge_pl_kernel(tc, keys, ka, kb, wd, offs, offs2, out_0, ou
             if t == 2:
                 pair_back(0, sums[0], pairs[0])
             if t < last:
-                scale_b(t, 0, J)
+                scale_b(t, 0, POOL)
+                scale_tail(t)
                 sum_turned(sums[t // 2][:, t % 2, :], t)
             if t == 1:
                 merge(x_first[:, :EARLY, :], 0, EARLY, 0, 2)
 
         scale_b(last, 0, HALF)
-        scale_b(last, HALF, J)
+        scale_b(last, HALF, POOL)
+        scale_tail(last)
         sum_turned(sums[1][:, 1, :], last)
-        deal_w(0, 0, PACK, 0, W_HALF, nc.scalar.copy)
+        deal_w(0, 0, PACK, 0, DEAL_S, nc.scalar.copy)
+        deal_w(0, 0, PACK, DEAL_S, W_HALF, nc.vector.tensor_copy)
+        deal_w(1, 0, PACK, 48, W_HALF, nc.scalar.copy)
+        deal_w(1, 0, 2, 0, 48, nc.scalar.copy)
         pair_back(1, sums[1], pairs[1])
-        deal_w(1, 0, 2, 0, DEAL_S, nc.scalar.copy)
-        deal_w(1, 2, PACK, 0, DEAL_S, nc.scalar.copy)
+        deal_w(1, 2, PACK, 0, 48, nc.scalar.copy)
         weave()
         merge(x_first[:, :EARLY, :], 0, EARLY, 2, PACK)
         merge(x_first[:, EARLY:, :], EARLY, HALF)
-        deal_w(1, 0, PACK, DEAL_S, W_HALF, nc.vector.tensor_copy)
         for j0 in range(0, HALF, CH):
             quant_x(0, j0, j0 + CH, x_first[:, j0 : j0 + CH, :])
 

@@ -26,7 +26,7 @@ LEAD = T // 4
 SPLIT = 176
 DEAL_S = 48
 POOL = 384
-EARLY = 192
+EARLY = 256
 
 
 def tile_attend_headmerge_pl_kernel(tc, keys, ka, kb, wd, offs, offs2, out_0, out_1, out_2):
@@ -41,7 +41,7 @@ def tile_attend_headmerge_pl_kernel(tc, keys, ka, kb, wd, offs, offs2, out_0, ou
         windows = [keep.tile([P, T], F32, name=f"window{t}") for t in range(PACK)]
         key_rows = keys.rearrange("(p t) n -> p t n", t=PACK)
         w_rows = wd.rearrange("(p r) c -> p r c", r=PACK)
-        w_second = keep.tile([P, PACK * C // 2 + P // 2], F32, name="w_second")
+        w_second = keep.tile([P, PACK * C // 2 + 3 * P // 4], F32, name="w_second")
         w_raw = [
             keep.tile([P, PACK, C // 2], F32, name="w_first")[:],
             w_second[:, : PACK * C // 2].rearrange("p (r c) -> p r c", r=PACK),
@@ -196,7 +196,7 @@ def tile_attend_headmerge_pl_kernel(tc, keys, ka, kb, wd, offs, offs2, out_0, ou
         sums = [psum.tile([P, 2, P], F32, name=f"sums{u}", tag=("turn0", "late3")[u]) for u in range(2)]
         pairs = [
             keep.tile([P, P, 2], BF16, name="pairs0")[:],
-            w_second[:, PACK * C // 2 - P // 2 :].bitcast(BF16).rearrange("j (p e) -> j p e", e=2),
+            w_second[:, PACK * C // 2 - P // 4 :].bitcast(BF16).rearrange("j (p e) -> j p e", e=2),
         ]
         last = PACK - 1
         for t in range(PACK):
@@ -217,15 +217,17 @@ def tile_attend_headmerge_pl_kernel(tc, keys, ka, kb, wd, offs, offs2, out_0, ou
         sum_turned(sums[1][:, 1, :], last)
         deal_w(0, 0, PACK, 0, DEAL_S, nc.scalar.copy)
         deal_w(0, 0, PACK, DEAL_S, W_HALF, nc.vector.tensor_copy)
-        deal_w(1, 0, PACK, 48, W_HALF, nc.scalar.copy)
-        deal_w(1, 0, 2, 0, 48, nc.scalar.copy)
+        deal_w(1, 0, PACK, 56, W_HALF, nc.scalar.copy)
+        deal_w(1, 0, 2, 0, 56, nc.scalar.copy)
         pair_back(1, sums[1], pairs[1])
-        deal_w(1, 2, PACK, 0, 48, nc.scalar.copy)
+        deal_w(1, 2, PACK, 0, 40, nc.scalar.copy)
         weave()
-        merge(x_first[:, :EARLY, :], 0, EARLY, 2, PACK)
-        merge(x_first[:, EARLY:, :], EARLY, HALF)
+        for j0 in range(0, HALF, CH):
+            merge(x_first[:, j0 : j0 + CH, :], j0, j0 + CH, 2, PACK)
         for j0 in range(0, HALF, CH):
             quant_x(0, j0, j0 + CH, x_first[:, j0 : j0 + CH, :])
+
+        deal_w(1, 2, PACK, 40, 56, nc.vector.tensor_copy)
 
         for t, tag in enumerate(("turn0", "first1", "first2", "first3")):
             quant_w(t)

from contextlib import ExitStack

import concourse.mybir as mybir
from concourse.masks import make_identity

D, T, J, C = 512, 2048, 512, 512
FLOPS = 2 * D * C * J

F32 = mybir.dt.float32
BF16 = mybir.dt.bfloat16
I32 = mybir.dt.int32
U16 = mybir.dt.uint16
U8 = mybir.dt.uint8
FP8X4 = mybir.dt.float8_e4m3fn_x4
MULT = mybir.AluOpType.mult
ADD = mybir.AluOpType.add
COPY = mybir.ActivationFunctionType.Copy

P = 128
PACK = 4
CH = 128
LINE = 4
HALF = J // 2
W_HALF = P // 2
LEAD = T // 4
SPLIT = 176
DEAL_S = 48
POOL = 384
EARLY = 256


def tile_attend_headmerge_pl_kernel(tc, keys, ka, kb, wd, offs, offs2, out_0, out_1, out_2):
    nc = tc.nc
    with ExitStack() as ctx:
        keep = ctx.enter_context(tc.tile_pool(name="keep", bufs=1))
        stage = ctx.enter_context(tc.tile_pool(name="stage", bufs=1))
        psum = ctx.enter_context(tc.psum_pool(name="psum", bufs=1))

        list_a = keep.tile([P, J // 16], U16, name="list_a")
        list_b = keep.tile([P, J // 16], U16, name="list_b")
        windows = [keep.tile([P, T], F32, name=f"window{t}") for t in range(PACK)]
        key_rows = keys.rearrange("(p t) n -> p t n", t=PACK)
        w_rows = wd.rearrange("(p r) c -> p r c", r=PACK)
        w_second = keep.tile([P, PACK * C // 2 + 3 * P // 4], F32, name="w_second")
        w_raw = [
            keep.tile([P, PACK, C // 2], F32, name="w_first")[:],
            w_second[:, : PACK * C // 2].rearrange("p (r c) -> p r c", r=PACK),
        ]
        term_a = keep.tile([P, PACK, J], F32, name="term_a")
        term_b = keep.tile([P, PACK, J], F32, name="term_b")
        raw_early = keep.tile([P, 3 * J], F32, name="raw_early")
        raw_last = stage.tile([P, J], F32, name="raw_last", align_bytes=64, offset=0)
        raw = [raw_early[:, :J], raw_early[:, J : 2 * J], raw_early[:, 2 * J :], raw_last[:]]
        cols = [keep.tile([P, PACK], F32, name="cols_a")[:], raw_early[:, J - 2 : J + 2]]

        nc.sync.dma_start(out=windows[0][:, :LEAD], in_=key_rows[:, 0, :LEAD])
        for s, share in enumerate((ka, kb)):
            nc.sync.dma_start(out=cols[s], in_=share.rearrange("o (p i) -> p (o i)", i=PACK))
        nc.sync.dma_start(list_a[:], offs)
        nc.sync.dma_start(list_b[:], offs2)
        nc.sync.dma_start(out=windows[0][:, LEAD:], in_=key_rows[:, 0, LEAD:])
        for t in range(1, PACK):
            nc.sync.dma_start(out=windows[t][:], in_=key_rows[:, t, :])
        for h in range(2):
            for r in range(0, PACK, 2):
                nc.sync.dma_start(out=w_raw[h][:, r : r + 2, :], in_=w_rows[:, r : r + 2, h * C // 2 : (h + 1) * C // 2])

        ident = keep.tile([P, P], F32, name="ident")
        make_identity(nc, ident[:])
        spread = [psum.tile([P, PACK, P], F32, name=f"spread{s}", tag=f"turn{s}") for s in range(2)]
        for s in range(2):
            for i in range(PACK):
                nc.tensor.transpose(spread[s][:, i, :], cols[s][:, i : i + 1].to_broadcast([P, P]), ident[:])
        share_a = keep.tile([P, J], F32, name="share_a")
        nc.scalar.copy(out=share_a[:].rearrange("m (p i) -> m p i", i=PACK), in_=spread[0][:].rearrange("m i p -> m p i"))
        share_b = spread[1][:].rearrange("m i p -> m p i")
        share_b_tail = keep.tile([P, J - POOL], F32, name="share_b_tail")
        nc.scalar.copy(out=share_b_tail[:].rearrange("m (p i) -> m p i", i=PACK), in_=share_b[:, POOL // PACK :, :])

        def gather_a(t):
            nc.vector.tensor_tensor(term_a[:, t, :], windows[t][:].indirect(list_a[:]), share_a[:], MULT)

        def gather_b(t):
            nc.scalar.activation(raw[t], windows[t][:].indirect(list_b[:]), COPY)

        def scale_b(t, j0, j1):
            nc.vector.tensor_tensor(
                term_b[:, t, j0:j1].rearrange("m (p i) -> m p i", i=PACK),
                raw[t][:, j0:j1].rearrange("m (p i) -> m p i", i=PACK),
                share_b[:, j0 // PACK : j1 // PACK, :],
                MULT,
            )

        def scale_tail(t):
            nc.gpsimd.tensor_tensor(term_b[:, t, POOL:], raw[t][:, POOL:], share_b_tail[:], MULT)

        x_first = keep.tile([P, HALF, PACK], BF16, name="x_first", align_bytes=64)
        x_turned = keep.tile([P, CH, PACK], BF16, name="x_turned", align_bytes=64)
        w_bf = keep.tile([P, PACK, P, PACK], BF16, name="w_bf", align_bytes=64)
        x_last = [w_bf[:, 2 * h, : CH // 2, :] for h in range(2)]
        turned = slice(HALF, HALF + CH)
        back = psum.tile([P, 2, CH], F32, name="back", tag="back")

        def sum_turned(dst, t):
            for s, term in enumerate((term_a, term_b)):
                nc.tensor.matmul(
                    dst, lhsT=term[:, t, turned], rhs=ident[:], is_transpose=True, start=(s == 0), stop=(s == 1)
                )

        def pair_back(u, bank, pair_tile):
            nc.scalar.copy(out=pair_tile, in_=bank[:].rearrange("j e p -> j p e"))
            nc.tensor.transpose(back[:, u, :], pair_tile.rearrange("j p e -> j (p e)").bitcast(F32), ident[:])

        def weave():
            pair_words = x_turned[:].rearrange("p j t -> p (j t)").bitcast(F32).rearrange("p (j u) -> p j u", u=2)
            nc.scalar.copy(out=pair_words, in_=back[:].rearrange("p u j -> p j u"))

        x_codes = [keep.tile([P, HALF], I32, name=f"x_codes{k}", align_bytes=64) for k in range(2)]
        x_scales = [keep.tile([P, HALF], U8, name=f"x_scales{k}", align_bytes=64) for k in range(2)]

        def merge(dst, j0, j1, t0=0, t1=PACK):
            nc.vector.tensor_tensor(
                dst[:, :, t0:t1].rearrange("p (g i) t -> p g t i", i=LINE),
                term_a[:, t0:t1, j0:j1].rearrange("p t (g i) -> p g t i", i=LINE),
                term_b[:, t0:t1, j0:j1].rearrange("p t (g i) -> p g t i", i=LINE),
                ADD,
            )

        def quant_x(k, j0, j1, src):
            nc.vector.quantize_mx(
                out=x_codes[k][:, j0:j1].bitcast(FP8X4),
                scales=x_scales[k][:, j0:j1],
                in_=src.rearrange("p j t -> p (j t)"),
            )

        w_codes = [keep.tile([P, 2 * P], I32, name=f"w_codes{u}", align_bytes=64) for u in range(2)]
        w_scales = [keep.tile([P, 2 * P], U8, name=f"w_scales{u}", align_bytes=64) for u in range(2)]

        def deal_w(h, t0, t1, m0, m1, move):
            move(
                out=w_bf[:, t0:t1, h * W_HALF + m0 : h * W_HALF + m1, :].rearrange("p t m r -> p m r t"),
                in_=w_raw[h].rearrange("p r (m t) -> p m r t", t=PACK)[:, m0:m1, :, t0:t1],
            )

        def quant_w(t):
            ms = slice(t % 2 * P, (t % 2 + 1) * P)
            nc.vector.quantize_mx(
                out=w_codes[t // 2][:, ms].bitcast(FP8X4),
                scales=w_scales[t // 2][:, ms],
                in_=w_bf[:, t, :, :].rearrange("p m r -> p (m r)"),
            )

        y_half = [keep.tile([P, PACK, HALF], F32, name=f"y_half{k}") for k in range(2)]
        y_bf = [keep.tile([P, HALF, PACK], BF16, name=f"y_bf{k}", align_bytes=64) for k in range(2)]
        y_codes = keep.tile([P, J], I32, name="y_codes", align_bytes=64)
        y_scales = keep.tile([P, J], U8, name="y_scales", align_bytes=64)
        y_rows = out_0.rearrange("(p t) j -> p t j", t=PACK)
        word_rows = out_1[0].rearrange("l c r -> l (c r)").bitcast(I32)
        scale_rows = out_2[0].bitcast(I32)

        def project(k, t, tag):
            ms = slice(t % 2 * P, (t % 2 + 1) * P)
            acc = psum.tile([P, HALF], F32, name=f"acc{k}{t}", tag=tag)
            nc.tensor.matmul_mx(
                out=acc[:],
                lhsT=w_codes[t // 2][:, ms].bitcast(FP8X4),
                lhsT_scale=w_scales[t // 2][:, ms],
                rhs=x_codes[k][:].bitcast(FP8X4),
                rhs_scale=x_scales[k][:],
                start=True,
                stop=True,
            )
            cuts = (0, CH, HALF) if t == PACK - 1 else (0, HALF)
            for j0, j1 in zip(cuts, cuts[1:]):
                nc.scalar.copy(out=y_half[k][:, t, j0:j1], in_=acc[:, j0:j1])

        def store(k, t0, t1):
            nc.sync.dma_start(out=y_rows[:, t0:t1, k * HALF : (k + 1) * HALF], in_=y_half[k][:, t0:t1, :])

        def round_y(k, j0, j1, move):
            move(
                out=y_bf[k][:, j0:j1, :].rearrange("p (g i) t -> p g t i", i=LINE),
                in_=y_half[k][:, :, j0:j1].rearrange("p t (g i) -> p g t i", i=LINE),
            )

        def planes_out(k):
            for j0 in range(0, HALF, CH):
                js = slice(k * HALF + j0, k * HALF + j0 + CH)
                nc.vector.quantize_mx(
                    out=y_codes[:, js].bitcast(FP8X4),
                    scales=y_scales[:, js],
                    in_=y_bf[k][:, j0 : j0 + CH, :].rearrange("p j t -> p (j t)"),
                )
            nc.sync.dma_start(out=word_rows[:, k * HALF : (k + 1) * HALF], in_=y_codes[:, k * HALF : (k + 1) * HALF])

        sums = [psum.tile([P, 2, P], F32, name=f"sums{u}", tag=("turn0", "late3")[u]) for u in range(2)]
        pairs = [
            keep.tile([P, P, 2], BF16, name="pairs0")[:],
            w_second[:, PACK * C // 2 - P // 4 :].bitcast(BF16).rearrange("j (p e) -> j p e", e=2),
        ]
        last = PACK - 1
        for t in range(PACK):
            gather_a(t)
            gather_b(t)
            if t == 2:
                pair_back(0, sums[0], pairs[0])
            if t < last:
                scale_b(t, 0, POOL)
                scale_tail(t)
                sum_turned(sums[t // 2][:, t % 2, :], t)
            if t == 1:
                merge(x_first[:, :EARLY, :], 0, EARLY, 0, 2)

        scale_b(last, 0, HALF)
        scale_b(last, HALF, POOL)
        scale_tail(last)
        sum_turned(sums[1][:, 1, :], last)
        deal_w(0, 0, PACK, 0, DEAL_S, nc.scalar.copy)
        deal_w(0, 0, PACK, DEAL_S, W_HALF, nc.vector.tensor_copy)
        deal_w(1, 0, PACK, 56, W_HALF, nc.scalar.copy)
        deal_w(1, 0, 2, 0, 56, nc.scalar.copy)
        pair_back(1, sums[1], pairs[1])
        deal_w(1, 2, PACK, 0, 40, nc.scalar.copy)
        weave()
        for j0 in range(0, HALF, CH):
            merge(x_first[:, j0 : j0 + CH, :], j0, j0 + CH, 2, PACK)
        for j0 in range(0, HALF, CH):
            quant_x(0, j0, j0 + CH, x_first[:, j0 : j0 + CH, :])

        deal_w(1, 2, PACK, 40, 56, nc.vector.tensor_copy)

        for t, tag in enumerate(("turn0", "first1", "first2", "first3")):
            quant_w(t)
            project(0, t, tag)
            if t:
                store(0, 0 if t == 1 else t, t + 1)
            if t % 2:
                j0 = HALF + CH + t // 2 * CH // 2
                merge(x_last[t // 2], j0, j0 + CH // 2)
        quant_x(1, 0, CH, x_turned[:])
        for h in range(2):
            quant_x(1, CH + h * CH // 2, CH + (h + 1) * CH // 2, x_last[h])

        for t, tag in enumerate(("turn1", "back", "late2", "late3")):
            project(1, t, tag)
            store(1, t, t + 1)

        round_y(0, 0, CH, nc.vector.tensor_copy)
        round_y(0, CH, HALF, nc.vector.tensor_copy)
        planes_out(0)
        round_y(1, 0, CH, nc.vector.tensor_copy)
        round_y(1, CH, SPLIT, nc.vector.tensor_copy)
        round_y(1, SPLIT, HALF, nc.scalar.copy)
        planes_out(1)

        for q in range(4):
            queue = nc.scalar if q % 2 else nc.sync
            queue.dma_start(out=scale_rows[4 * q : 4 * q + 4, :], in_=y_scales[32 * q : 32 * q + 4, :].bitcast(I32))
